import numpy as np
import ml_dtypes


def mxq(x, axis, fmt="e4m3"):
    dtype, down = {"e4m3": (ml_dtypes.float8_e4m3fn, 7), "e5m2": (ml_dtypes.float8_e5m2, 14)}[fmt]
    v = np.moveaxis(np.asarray(x, np.float32).astype(ml_dtypes.bfloat16).astype(np.float64), axis, -1)
    blocks = v.reshape(v.shape[:-1] + (-1, 32))
    amax = np.abs(blocks).max(-1, keepdims=True)
    byte = np.maximum(np.where(amax > 0, np.frexp(amax)[1] - 1 + 127, 0) - down, 1)
    scale = np.exp2(byte - 127.0)
    codes = (blocks / scale).astype(np.float32).astype(dtype).astype(np.float64)
    return np.moveaxis((codes * scale).reshape(v.shape), -1, axis)


WIDE = False


def mx_kscale(k):
    if not WIDE:
        return np.ones(k)
    levels = np.array([10, -10, 5, -5, 0])
    if k % 512:
        return np.exp2(np.random.permutation(np.resize(levels, k // 32))).repeat(32)
    a = np.empty((k // 512, 16))
    for p in range(k // 512):
        a[p, :8] = np.random.permutation(np.resize(levels, 8))
        for g in range(8):
            far = levels[np.abs(levels - a[p, g]) >= 10]
            a[p, g + 8] = far[np.random.randint(len(far))]
    return np.exp2(a.ravel()).repeat(32)


def f64(x):
    return np.asarray(x).astype(np.float64)


def striped(idx):
    return np.tile(idx.reshape(-1, 16).T, (8, 1)).astype(np.uint16)


def unstriped(offs):
    return offs[:16].T.reshape(-1).astype(np.int64)


E2M1 = np.array([0.0, 0.5, 1.0, 1.5, 2.0, 3.0, 4.0, 6.0, -0.0, -0.5, -1.0, -1.5, -2.0, -3.0, -4.0, -6.0])


def pack_weight(w, fmt):
    k, n = w.shape
    w = f64(np.asarray(w, np.float32).astype(ml_dtypes.bfloat16)).reshape(k // 32, 32, n)
    amax = np.abs(w).max(1)
    if fmt == "e4m3":
        byte = np.frexp(amax)[1] - 1 + 127 - 7
    else:
        mant, ex = np.frexp(amax / 6.0)
        byte = np.where(mant > 0.5, ex, ex - 1) + 127
    byte = np.clip(np.where(amax > 0, byte, 1), 1, 254)
    scaled = (w * np.exp2(127.0 - byte)[:, None, :]).reshape(k, n).astype(np.float32)
    by_word = np.ascontiguousarray(scaled.reshape(k // 512, 128, 4, n).transpose(0, 1, 3, 2))
    if fmt == "e4m3":
        words = by_word.astype(ml_dtypes.float8_e4m3fn).view(np.uint8)
    else:
        c = by_word.astype(ml_dtypes.float4_e2m1fn).view(np.uint8) & 0xF
        words = (c[..., 0::2] | (c[..., 1::2] << 4)).reshape(k // 512, 128, 2 * n)
    return np.ascontiguousarray(words), np.ascontiguousarray(byte.astype(np.uint8).reshape(k // 512, 16, n))


def unpack_weight(words, scales, fmt):
    g, _, n = scales.shape
    words = np.ascontiguousarray(words).reshape(g, 128, n, -1)
    if fmt == "e4m3":
        vals = words.view(ml_dtypes.float8_e4m3fn).astype(np.float64)
    else:
        nib = np.empty((g, 128, n, 4), np.uint8)
        nib[..., 0::2] = words & 0xF
        nib[..., 1::2] = words >> 4
        vals = E2M1[nib]
    vals = vals * np.repeat(np.exp2(scales.astype(np.float64) - 127.0), 8, axis=1)[..., None]
    return vals.transpose(0, 1, 3, 2).reshape(g * 512, n)


def silu(v):
    return v / (1.0 + np.exp(-np.maximum(v, -700.0)))


K, T, E, C, H, N = 512, 512, 4, 256, 1024, 128


def by_expert(wq, xq):
    return np.concatenate([wq[e].T @ xq[:, e * C:(e + 1) * C] for e in range(E)], axis=1)


def setup_inputs():
    n = np.random.standard_normal
    s = mx_kscale(K)[:, None]
    u = mx_kscale(H)
    first = np.random.permutation(np.repeat(np.arange(E), T // E))
    second = (first + 1 + np.random.permutation(np.repeat(np.arange(E - 1), -(-T // (E - 1)))[:T])) % E
    while np.bincount(second, minlength=E).max() != T // E:
        load = np.bincount(second, minlength=E); hi, lo = int(load.argmax()), int(load.argmin())
        t = np.flatnonzero((second == hi) & (first != lo))[0]; second[t] = lo
    slot_token = np.empty(E * C, np.int64); pos = np.empty((2, T), np.int64); fill = np.zeros(E, np.int64)
    place = np.stack([np.random.permutation(C) for _ in range(E)])
    for r, deal in enumerate((first, second)):
        for t in np.random.permutation(T):
            e = deal[t]; j = e * C + place[e, fill[e]]; fill[e] += 1; slot_token[j] = t; pos[r, t] = j
    g = np.random.uniform(0.2, 0.8, T)
    w1 = [pack_weight(m, "e2m1") for m in n((E, K, H)) / np.sqrt(K) / s[None]]
    w3 = [pack_weight(m, "e2m1") for m in n((E, K, H)) / np.sqrt(K) / s[None] * u[None, None, :]]
    w2 = [pack_weight(m, "e2m1") for m in n((E, H, N)) / np.sqrt(H) / u[None, :, None]]
    w_slot = np.empty(E * C); w_slot[pos[0]] = g; w_slot[pos[1]] = 1.0 - g
    return {
        "xT": (n((K, T)) * s).astype(np.float32),
        "w1_words": np.stack([m[0] for m in w1]),
        "w1_scales": np.stack([m[1] for m in w1]),
        "w3_words": np.stack([m[0] for m in w3]),
        "w3_scales": np.stack([m[1] for m in w3]),
        "w2_words": np.stack([m[0] for m in w2]),
        "w2_scales": np.stack([m[1] for m in w2]),
        "gate": np.tile(w_slot, (K, 1)).astype(np.float32),
        "offs": striped(slot_token),
        "pos1": striped(pos[0]),
        "pos2": striped(pos[1]),
    }


def reference(xT, w1_words, w1_scales, w3_words, w3_scales, w2_words, w2_scales, gate, offs, pos1, pos2):
    idx = unstriped(offs)
    w1 = np.stack([unpack_weight(w1_words[e], w1_scales[e], "e2m1") for e in range(E)])
    w3 = np.stack([unpack_weight(w3_words[e], w3_scales[e], "e2m1") for e in range(E)])
    w2 = np.stack([unpack_weight(w2_words[e], w2_scales[e], "e2m1") for e in range(E)])
    xq = mxq(f64(gate) * f64(xT)[:, idx], 0, "e4m3")
    h = silu(by_expert(w1, xq))
    h = h * by_expert(w3, xq)
    y = by_expert(w2, mxq(h, 0, "e4m3"))
    return y[:, unstriped(pos1)] + y[:, unstriped(pos2)]

@@ -1,0 +1,235 @@
+from contextlib import ExitStack
+
+import concourse.mybir as mybir
+from concourse.masks import make_identity
+
+K, T, E, C, H, N = 512, 512, 4, 256, 1024, 128
+S = E * C
+FLOPS = 2 * S * (2 * K * H + H * N)
+BYTES = 4 * K * T + 4 * 128 * S + E * (2 * K * H + H * N) * 17 // 32 + 2 * 128 * (S + 2 * T) // 16 + 4 * N * T
+
+F32 = mybir.dt.float32
+BF16 = mybir.dt.bfloat16
+I32 = mybir.dt.int32
+U32 = mybir.dt.uint32
+U16 = mybir.dt.uint16
+U8 = mybir.dt.uint8
+FP8X4 = mybir.dt.float8_e4m3fn_x4
+FP4X4 = mybir.dt.float4_e2m1fn_x4
+MULT = mybir.AluOpType.mult
+ADD = mybir.AluOpType.add
+SILU = mybir.ActivationFunctionType.Silu
+
+P = 128
+PACK = 4
+PASS = P * PACK
+HP = H // PASS
+TILES = S // P
+PER = 16
+
+
+def tile_moe_pre_glu_silu_kernel(
+    tc, xT, w1_words, w1_scales, w3_words, w3_scales, w2_words, w2_scales, gate, offs, pos1, pos2, out
+):
+    nc = tc.nc
+    with ExitStack() as ctx:
+        keep = ctx.enter_context(tc.tile_pool(name="keep", bufs=1))
+        work = ctx.enter_context(tc.tile_pool(name="work", bufs=3))
+        psum = ctx.enter_context(tc.psum_pool(name="psum", bufs=1))
+
+        offs_t = keep.tile([P, S // PER], U16, name="offs_t")
+        pos1_t = keep.tile([P, T // PER], U16, name="pos1_t")
+        pos2_t = keep.tile([P, T // PER], U16, name="pos2_t")
+        x_rows = [keep.tile([P, T], F32, name="x_rows%d" % d) for d in range(PACK)]
+        gate_t = keep.tile([P, S], F32, name="gate_t")
+        w1_t = keep.tile([P, E, 2 * H], U8, name="w1_t", align_bytes=64)
+        w3_t = keep.tile([P, E, 2 * H], U8, name="w3_t", align_bytes=64)
+        w2_t = keep.tile([P, E * HP, 2 * N], U8, name="w2_t", align_bytes=64)
+        s1_t = keep.tile([P, E, H], U8, name="s1_t", align_bytes=64)
+        s3_t = keep.tile([P, E, H], U8, name="s3_t", align_bytes=64)
+        warm = keep.tile([P, 2], F32, name="warm")
+        s2_t = keep.tile([P, E * HP, N], U8, name="s2_t", align_bytes=64)
+        ident = keep.tile([P, P], F32, name="ident")
+        y_all = keep.tile([P, S], F32, name="y_all")
+
+        def load_scales(queue, plane, scales, lo, hi):
+            rows = scales.rearrange("e s (q r) n -> r q (e s) n", r=4)
+            for r in range(4):
+                queue.dma_start(out=plane[r:P:32, lo:hi, :].bitcast(I32), in_=rows[r][:, lo:hi, :].bitcast(I32))
+
+        def load_words(tile, words, lo, hi):
+            nc.sync.dma_start(out=tile[:, lo:hi, :].bitcast(I32), in_=words.rearrange("e s p n -> p (e s) n")[:, lo:hi, :].bitcast(I32))
+
+        x_by_d = xT.rearrange("(p d) t -> d p t", d=PACK)
+        nc.scalar.dma_start(out=gate_t[:, 0:C], in_=gate[0:P, 0:C])
+        nc.gpsimd.memset(warm[:, 0:1], 0.0)
+        nc.scalar.activation(out=warm[:, 1:2], in_=warm[:, 0:1], func=SILU)
+        for plane, lo, hi in ((s1_t, 0, 1), (s3_t, 0, 1), (s1_t, 1, E), (s3_t, 1, E), (s2_t, 0, E * HP)):
+            nc.vector.memset(plane[:, lo:hi, :].rearrange("p a n -> p (a n)").bitcast(I32), 0)
+        nc.sync.dma_start(offs_t[:], offs)
+        nc.sync.dma_start(out=x_rows[0][:], in_=x_by_d[0])
+        for d in range(1, PACK):
+            nc.sync.dma_start(out=x_rows[d][:], in_=x_by_d[d])
+        load_scales(nc.gpsimd, s1_t, w1_scales, 0, 1)
+        load_scales(nc.scalar, s3_t, w3_scales, 0, 1)
+        nc.sync.dma_start(out=gate_t[:, C:2 * C], in_=gate[0:P, C:2 * C])
+        load_words(w1_t, w1_words, 0, 1)
+        load_words(w3_t, w3_words, 0, 1)
+        nc.sync.dma_start(out=gate_t[:, 2 * C:S], in_=gate[0:P, 2 * C:S])
+        load_words(w1_t, w1_words, 1, 2)
+        load_words(w3_t, w3_words, 1, 2)
+        load_scales(nc.sync, s3_t, w3_scales, 1, 4)
+        load_words(w2_t, w2_words, 0, E * HP)
+        load_scales(nc.sync, s2_t, w2_scales, 0, 8)
+        load_words(w1_t, w1_words, 2, E)
+        load_words(w3_t, w3_words, 2, E)
+        nc.sync.dma_start(pos1_t[:], pos1)
+        nc.sync.dma_start(pos2_t[:], pos2)
+        make_identity(nc, ident[:])
+        load_scales(nc.gpsimd, s1_t, w1_scales, 1, 4)
+
+        def gather(g, d, e, lo, hi):
+            a, b = e * C + lo, e * C + hi
+            nc.vector.tensor_tensor(g[:, d, lo:hi], x_rows[d][:].indirect(offs_t[:, a // PER:b // PER]), gate_t[:, a:b], MULT)
+
+        def round_x(g, lo, hi):
+            xb = work.tile([P, (hi - lo) * PACK], BF16, name="xb", align_bytes=64, bufs=3)
+            nc.scalar.copy(
+                out=xb[:].rearrange("p (c i d) -> p c d i", i=2, d=PACK),
+                in_=g[:, :, lo:hi].rearrange("p d (c i) -> p c d i", i=2),
+            )
+            return xb
+
+        def quantise(values, width, name, bufs):
+            codes = work.tile([P, width], U32, name=name + "_codes", align_bytes=64, bufs=bufs)
+            scales = work.tile([P, width], U8, name=name + "_scales", align_bytes=64, bufs=bufs)
+            nc.vector.quantize_mx(out=codes[:].bitcast(FP8X4), scales=scales[:], in_=values[:])
+            return codes, scales
+
+        x_mx = {}
+
+        def prepare_tile(j):
+            g = work.tile([P, PACK, P], F32, name="g", bufs=3)
+            for d in range(PACK):
+                nc.vector.tensor_tensor(g[:, d, :], x_rows[d][:].indirect(offs_t[:, j * P // PER:(j + 1) * P // PER]), gate_t[:, j * P:(j + 1) * P], MULT)
+            codes, scales = quantise(round_x(g, 0, P), P, "x", 2)
+            x_mx[j] = (codes[:], scales[:])
+
+        def prepare(e):
+            g = work.tile([P, PACK, C], F32, name="g", bufs=3)
+            if e == 0:
+                for d in range(PACK - 1):
+                    gather(g, d, e, 0, C)
+                for c in range(2):
+                    gather(g, PACK - 1, e, c * P, (c + 1) * P)
+                    codes, scales = quantise(round_x(g, c * P, (c + 1) * P), P, "x", 2)
+                    x_mx[c] = (codes[:], scales[:])
+            else:
+                for d in range(PACK):
+                    gather(g, d, e, 0, C)
+                codes, scales = quantise(round_x(g, 0, C), C, "x", 2)
+                for c in range(2):
+                    x_mx[2 * e + c] = (codes[:, c * P:(c + 1) * P], scales[:, c * P:(c + 1) * P])
+
+        def first_layer(j, s):
+            e = j // 2
+            codes, scales = x_mx[j]
+            a = psum.tile([P, PASS], F32, name="a", bufs=2)
+            b = psum.tile([P, PASS], F32, name="b", bufs=3)
+            for acc, w, sc in ((a, w1_t[:, e, :], s1_t[:, e, :]), (b, w3_t[:, e, :], s3_t[:, e, :])):
+                nc.tensor.matmul_mx(
+                    out=acc[:], lhsT=codes.bitcast(FP8X4), lhsT_scale=scales,
+                    rhs=w[:, 2 * PASS * s:2 * PASS * (s + 1)].bitcast(FP4X4), rhs_scale=sc[:, PASS * s:PASS * (s + 1)],
+                    start=True, stop=True,
+                )
+            act = work.tile([P, PASS], F32, name="act", bufs=6)
+            nc.scalar.activation(
+                out=act[:].rearrange("j (u p v) -> j u p v", u=2, v=2),
+                in_=a[:].rearrange("j (p u v) -> j u p v", u=2, v=2), func=SILU,
+            )
+            h = work.tile([P, PASS], BF16, name="h", bufs=6)
+            nc.vector.tensor_tensor(
+                h[:].rearrange("j (u p v) -> j u p v", u=2, v=2),
+                act[:].rearrange("j (u p v) -> j u p v", u=2, v=2),
+                b[:].rearrange("j (p u v) -> j u p v", u=2, v=2), MULT,
+            )
+            return h
+
+        def turn(hs):
+            n = len(hs)
+            turned = psum.tile([P, n, 2, P], F32, name="turned", bufs=2)
+            for s, h in enumerate(hs):
+                pairs = h[:].bitcast(F32)
+                for u in range(2):
+                    nc.tensor.transpose(turned[:, s, u, :], pairs[:, u * P:(u + 1) * P], ident[:])
+            hb = work.tile([P, n * PASS], BF16, name="hb", align_bytes=64)
+            nc.scalar.copy(
+                out=hb[:].bitcast(F32).rearrange("p (s j u) -> p s j u", s=n, u=2),
+                in_=turned[:].rearrange("p s u j -> p s j u"),
+            )
+            codes, scales = quantise(hb, n * P, "h", 4)
+            return [(codes[:, s * P:(s + 1) * P], scales[:, s * P:(s + 1) * P]) for s in range(n)]
+
+        def second_layer(j, h_mx):
+            e = j // 2
+            y = psum.tile([P, P], F32, name="y", bufs=1)
+            for s in range(HP):
+                codes, scales = h_mx[s]
+                nc.tensor.matmul_mx(
+                    out=y[:], lhsT=w2_t[:, e * HP + s, :].bitcast(FP4X4), lhsT_scale=s2_t[:, e * HP + s, :],
+                    rhs=codes.bitcast(FP8X4), rhs_scale=scales, start=(s == 0), stop=(s == HP - 1),
+                )
+            nc.scalar.copy(out=y_all[:, j * P:(j + 1) * P], in_=y[:])
+
+        hs, h_mx = {}, {}
+        prepare_tile(0)
+        prepare_tile(1)
+        hs[0] = [first_layer(0, 0)]
+        hs[0].append(first_layer(0, 1))
+        prepare_tile(2)
+        hs[1] = [first_layer(1, 0)]
+        hs[1].append(first_layer(1, 1))
+        h_mx[0] = turn(hs[0])
+        prepare_tile(3)
+        hs[2] = [first_layer(2, 0)]
+        hs[2].append(first_layer(2, 1))
+        h_mx[1] = turn(hs[1])
+        second_layer(0, h_mx[0])
+        prepare_tile(4)
+        hs[3] = [first_layer(3, 0)]
+        hs[3].append(first_layer(3, 1))
+        h_mx[2] = turn(hs[2])
+        second_layer(1, h_mx[1])
+        prepare_tile(5)
+        hs[4] = [first_layer(4, 0)]
+        hs[4].append(first_layer(4, 1))
+        h_mx[3] = turn(hs[3])
+        second_layer(2, h_mx[2])
+        prepare_tile(6)
+        hs[5] = [first_layer(5, 0)]
+        hs[5].append(first_layer(5, 1))
+        h_mx[4] = turn(hs[4])
+        second_layer(3, h_mx[3])
+        prepare_tile(7)
+        hs[6] = [first_layer(6, 0)]
+        hs[6].append(first_layer(6, 1))
+        h_mx[5] = turn(hs[5])
+        second_layer(4, h_mx[4])
+        hs[7] = [first_layer(7, 0)]
+        hs[7].append(first_layer(7, 1))
+        h_mx[6] = turn(hs[6])
+        second_layer(5, h_mx[5])
+        early = turn(hs[7][:1])
+        second_layer(6, h_mx[6])
+        second_layer(7, early + turn(hs[7][1:]))
+
+        half = T // 2
+        for c in range(2):
+            cols = slice(c * half // PER, (c + 1) * half // PER)
+            y1 = work.tile([P, half], F32, name="y1")
+            y2 = work.tile([P, half], F32, name="y2")
+            total = work.tile([P, half], F32, name="total")
+            nc.vector.tensor_copy(y1[:], y_all[:].indirect(pos1_t[:, cols]))
+            nc.vector.tensor_copy(y2[:], y_all[:].indirect(pos2_t[:, cols]))
+            nc.vector.tensor_tensor(total[:], y1[:], y2[:], ADD)
+            nc.sync.dma_start(out=out[:, c * half:(c + 1) * half], in_=total[:])

@@ -4,9 +4,29 @@ import concourse.mybir as mybir
 from concourse.masks import make_identity
 
 K, T, E, C, H, N = 512, 512, 4, 256, 1024, 128
-S = E * C
-FLOPS = 2 * S * (2 * K * H + H * N)
-BYTES = 4 * K * T + 4 * 128 * S + E * (2 * K * H + H * N) * 17 // 32 + 2 * 128 * (S + 2 * T) // 16 + 4 * N * T
+SLOTS = E * C
+P = 128
+PACK = 4
+PASS = P * PACK
+H_PASSES = H // PASS
+TILES_PER_EXPERT = C // P
+TILES = SLOTS // P
+UNITS = TILES * H_PASSES
+PER_COLUMN = 16
+QUADRANT = 32
+SCALE_ROWS = 4
+
+FLOPS = 2 * SLOTS * (2 * K * H + H * N)
+BYTES = 4 * K * T + 4 * P * SLOTS + E * (2 * K * H + H * N) * 17 // 32 + 2 * P * (SLOTS + 2 * T) // PER_COLUMN + 4 * N * T
+
+ACT_LEAD = 2
+TURN_LAG = 2
+SECOND_LAG = 4
+PAIRED_TILES = 4
+TURNED_BY_VECTOR = TILES - 2
+
+A_BANKS, B_BANKS, TURN_BANKS, Y_BANKS = 3, 2, 2, 1
+X_ROUNDED_BUFS, X_MX_BUFS, ACT_BUFS, H_BUFS, H_TURNED_BUFS, H_MX_BUFS, RESULT_BUFS = 3, 2, 6, 12, 4, 6, 2
 
 F32 = mybir.dt.float32
 BF16 = mybir.dt.bfloat16
@@ -20,13 +40,6 @@ MULT = mybir.AluOpType.mult
 ADD = mybir.AluOpType.add
 SILU = mybir.ActivationFunctionType.Silu
 
-P = 128
-PACK = 4
-PASS = P * PACK
-HP = H // PASS
-TILES = S // P
-PER = 16
-
 
 def tile_moe_pre_glu_silu_kernel(
     tc, xT, w1_words, w1_scales, w3_words, w3_scales, w2_words, w2_scales, gate, offs, pos1, pos2, out
@@ -34,202 +47,185 @@ def tile_moe_pre_glu_silu_kernel(
     nc = tc.nc
     with ExitStack() as ctx:
         keep = ctx.enter_context(tc.tile_pool(name="keep", bufs=1))
-        work = ctx.enter_context(tc.tile_pool(name="work", bufs=3))
+        work = ctx.enter_context(tc.tile_pool(name="work", bufs=1))
         psum = ctx.enter_context(tc.psum_pool(name="psum", bufs=1))
 
-        offs_t = keep.tile([P, S // PER], U16, name="offs_t")
-        pos1_t = keep.tile([P, T // PER], U16, name="pos1_t")
-        pos2_t = keep.tile([P, T // PER], U16, name="pos2_t")
+        offs_sb = keep.tile([P, SLOTS // PER_COLUMN], U16, name="offs_sb")
+        pos1_sb = keep.tile([P, T // PER_COLUMN], U16, name="pos1_sb")
+        pos2_sb = keep.tile([P, T // PER_COLUMN], U16, name="pos2_sb")
         x_rows = [keep.tile([P, T], F32, name="x_rows%d" % d) for d in range(PACK)]
-        gate_t = keep.tile([P, S], F32, name="gate_t")
-        w1_t = keep.tile([P, E, 2 * H], U8, name="w1_t", align_bytes=64)
-        w3_t = keep.tile([P, E, 2 * H], U8, name="w3_t", align_bytes=64)
-        w2_t = keep.tile([P, E * HP, 2 * N], U8, name="w2_t", align_bytes=64)
-        s1_t = keep.tile([P, E, H], U8, name="s1_t", align_bytes=64)
-        s3_t = keep.tile([P, E, H], U8, name="s3_t", align_bytes=64)
+        gate_sb = keep.tile([P, SLOTS], F32, name="gate_sb")
+        w1_sb = keep.tile([P, E, 2 * H], U8, name="w1_sb", align_bytes=64)
+        w3_sb = keep.tile([P, E, 2 * H], U8, name="w3_sb", align_bytes=64)
+        w2_sb = keep.tile([P, E * H_PASSES, 2 * N], U8, name="w2_sb", align_bytes=64)
+        s1_sb = keep.tile([P, E, H], U8, name="s1_sb", align_bytes=64)
+        s3_sb = keep.tile([P, E, H], U8, name="s3_sb", align_bytes=64)
+        s2_sb = keep.tile([P, E * H_PASSES, N], U8, name="s2_sb", align_bytes=64)
+        gathered = [keep.tile([P, PACK, PASS], F32, name="gathered%d" % e) for e in range(E)]
+        identity = keep.tile([P, P], F32, name="identity")
+        y_sb = keep.tile([P, SLOTS], F32, name="y_sb")
         warm = keep.tile([P, 2], F32, name="warm")
-        s2_t = keep.tile([P, E * HP, N], U8, name="s2_t", align_bytes=64)
-        ident = keep.tile([P, P], F32, name="ident")
-        y_all = keep.tile([P, S], F32, name="y_all")
-
-        def load_scales(queue, plane, scales, lo, hi):
-            rows = scales.rearrange("e s (q r) n -> r q (e s) n", r=4)
-            for r in range(4):
-                queue.dma_start(out=plane[r:P:32, lo:hi, :].bitcast(I32), in_=rows[r][:, lo:hi, :].bitcast(I32))
 
         def load_words(tile, words, lo, hi):
-            nc.sync.dma_start(out=tile[:, lo:hi, :].bitcast(I32), in_=words.rearrange("e s p n -> p (e s) n")[:, lo:hi, :].bitcast(I32))
+            by_pass = words.rearrange("e s p n -> p (e s) n")
+            nc.sync.dma_start(out=tile[:, lo:hi, :].bitcast(I32), in_=by_pass[:, lo:hi, :].bitcast(I32))
 
-        x_by_d = xT.rearrange("(p d) t -> d p t", d=PACK)
-        nc.scalar.dma_start(out=gate_t[:, 0:C], in_=gate[0:P, 0:C])
+        def load_scales(tile, scales):
+            rows = scales.rearrange("e s (q r) n -> r q (e s) n", r=SCALE_ROWS)
+            for r in range(SCALE_ROWS):
+                nc.sync.dma_start(out=tile[r:P:QUADRANT, :, :].bitcast(I32), in_=rows[r].bitcast(I32))
+
+        def load_gate(lo, hi):
+            nc.sync.dma_start(out=gate_sb[:, lo:hi], in_=gate[0:P, lo:hi])
+
+        for tile in (s1_sb, s3_sb, s2_sb):
+            nc.vector.memset(tile[:].rearrange("p a n -> p (a n)").bitcast(I32), 0)
         nc.gpsimd.memset(warm[:, 0:1], 0.0)
         nc.scalar.activation(out=warm[:, 1:2], in_=warm[:, 0:1], func=SILU)
-        for plane, lo, hi in ((s1_t, 0, 1), (s3_t, 0, 1), (s1_t, 1, E), (s3_t, 1, E), (s2_t, 0, E * HP)):
-            nc.vector.memset(plane[:, lo:hi, :].rearrange("p a n -> p (a n)").bitcast(I32), 0)
-        nc.sync.dma_start(offs_t[:], offs)
+
+        x_by_d = xT.rearrange("(p d) t -> d p t", d=PACK)
+        nc.sync.dma_start(offs_sb[:], offs)
         nc.sync.dma_start(out=x_rows[0][:], in_=x_by_d[0])
+        load_gate(0, C)
         for d in range(1, PACK):
             nc.sync.dma_start(out=x_rows[d][:], in_=x_by_d[d])
-        load_scales(nc.gpsimd, s1_t, w1_scales, 0, 1)
-        load_scales(nc.scalar, s3_t, w3_scales, 0, 1)
-        nc.sync.dma_start(out=gate_t[:, C:2 * C], in_=gate[0:P, C:2 * C])
-        load_words(w1_t, w1_words, 0, 1)
-        load_words(w3_t, w3_words, 0, 1)
-        nc.sync.dma_start(out=gate_t[:, 2 * C:S], in_=gate[0:P, 2 * C:S])
-        load_words(w1_t, w1_words, 1, 2)
-        load_words(w3_t, w3_words, 1, 2)
-        load_scales(nc.sync, s3_t, w3_scales, 1, 4)
-        load_words(w2_t, w2_words, 0, E * HP)
-        load_scales(nc.sync, s2_t, w2_scales, 0, 8)
-        load_words(w1_t, w1_words, 2, E)
-        load_words(w3_t, w3_words, 2, E)
-        nc.sync.dma_start(pos1_t[:], pos1)
-        nc.sync.dma_start(pos2_t[:], pos2)
-        make_identity(nc, ident[:])
-        load_scales(nc.gpsimd, s1_t, w1_scales, 1, 4)
+        load_gate(C, 2 * C)
+        load_words(w1_sb, w1_words, 0, 1)
+        load_scales(s1_sb, w1_scales)
+        load_gate(2 * C, SLOTS)
+        load_words(w3_sb, w3_words, 0, 1)
+        load_scales(s3_sb, w3_scales)
+        load_words(w1_sb, w1_words, 1, 2)
+        load_words(w3_sb, w3_words, 1, 2)
+        load_words(w2_sb, w2_words, 0, E * H_PASSES)
+        load_scales(s2_sb, w2_scales)
+        load_words(w1_sb, w1_words, 2, E)
+        load_words(w3_sb, w3_words, 2, E)
+        nc.sync.dma_start(pos1_sb[:], pos1)
+        nc.sync.dma_start(pos2_sb[:], pos2)
+        make_identity(nc, identity[:])
 
-        def gather(g, d, e, lo, hi):
-            a, b = e * C + lo, e * C + hi
-            nc.vector.tensor_tensor(g[:, d, lo:hi], x_rows[d][:].indirect(offs_t[:, a // PER:b // PER]), gate_t[:, a:b], MULT)
-
-        def round_x(g, lo, hi):
-            xb = work.tile([P, (hi - lo) * PACK], BF16, name="xb", align_bytes=64, bufs=3)
-            nc.scalar.copy(
-                out=xb[:].rearrange("p (c i d) -> p c d i", i=2, d=PACK),
-                in_=g[:, :, lo:hi].rearrange("p d (c i) -> p c d i", i=2),
-            )
-            return xb
+        x_mx, act_of, h_of, turned_of, h_mx, y_bank = {}, {}, {}, {}, {}, {}
 
         def quantise(values, width, name, bufs):
             codes = work.tile([P, width], U32, name=name + "_codes", align_bytes=64, bufs=bufs)
             scales = work.tile([P, width], U8, name=name + "_scales", align_bytes=64, bufs=bufs)
-            nc.vector.quantize_mx(out=codes[:].bitcast(FP8X4), scales=scales[:], in_=values[:])
-            return codes, scales
+            nc.vector.quantize_mx(out=codes[:].bitcast(FP8X4), scales=scales[:], in_=values)
+            return [(codes[:, c:c + P].bitcast(FP8X4), scales[:, c:c + P]) for c in range(0, width, P)]
 
-        x_mx = {}
+        def gather(e, d, lo=0, hi=C):
+            first, end = e * C + lo, e * C + hi
+            tokens = x_rows[d][:].indirect(offs_sb[:, first // PER_COLUMN:end // PER_COLUMN])
+            nc.vector.tensor_tensor(gathered[e][:, d, lo:hi], tokens, gate_sb[:, first:end], MULT)
 
-        def prepare_tile(j):
-            g = work.tile([P, PACK, P], F32, name="g", bufs=3)
-            for d in range(PACK):
-                nc.vector.tensor_tensor(g[:, d, :], x_rows[d][:].indirect(offs_t[:, j * P // PER:(j + 1) * P // PER]), gate_t[:, j * P:(j + 1) * P], MULT)
-            codes, scales = quantise(round_x(g, 0, P), P, "x", 2)
-            x_mx[j] = (codes[:], scales[:])
-
-        def prepare(e):
-            g = work.tile([P, PACK, C], F32, name="g", bufs=3)
-            if e == 0:
-                for d in range(PACK - 1):
-                    gather(g, d, e, 0, C)
-                for c in range(2):
-                    gather(g, PACK - 1, e, c * P, (c + 1) * P)
-                    codes, scales = quantise(round_x(g, c * P, (c + 1) * P), P, "x", 2)
-                    x_mx[c] = (codes[:], scales[:])
-            else:
-                for d in range(PACK):
-                    gather(g, d, e, 0, C)
-                codes, scales = quantise(round_x(g, 0, C), C, "x", 2)
-                for c in range(2):
-                    x_mx[2 * e + c] = (codes[:, c * P:(c + 1) * P], scales[:, c * P:(c + 1) * P])
-
-        def first_layer(j, s):
-            e = j // 2
-            codes, scales = x_mx[j]
-            a = psum.tile([P, PASS], F32, name="a", bufs=2)
-            b = psum.tile([P, PASS], F32, name="b", bufs=3)
-            for acc, w, sc in ((a, w1_t[:, e, :], s1_t[:, e, :]), (b, w3_t[:, e, :], s3_t[:, e, :])):
-                nc.tensor.matmul_mx(
-                    out=acc[:], lhsT=codes.bitcast(FP8X4), lhsT_scale=scales,
-                    rhs=w[:, 2 * PASS * s:2 * PASS * (s + 1)].bitcast(FP4X4), rhs_scale=sc[:, PASS * s:PASS * (s + 1)],
-                    start=True, stop=True,
-                )
-            act = work.tile([P, PASS], F32, name="act", bufs=6)
-            nc.scalar.activation(
-                out=act[:].rearrange("j (u p v) -> j u p v", u=2, v=2),
-                in_=a[:].rearrange("j (p u v) -> j u p v", u=2, v=2), func=SILU,
-            )
-            h = work.tile([P, PASS], BF16, name="h", bufs=6)
-            nc.vector.tensor_tensor(
-                h[:].rearrange("j (u p v) -> j u p v", u=2, v=2),
-                act[:].rearrange("j (u p v) -> j u p v", u=2, v=2),
-                b[:].rearrange("j (p u v) -> j u p v", u=2, v=2), MULT,
-            )
-            return h
-
-        def turn(hs):
-            n = len(hs)
-            turned = psum.tile([P, n, 2, P], F32, name="turned", bufs=2)
-            for s, h in enumerate(hs):
-                pairs = h[:].bitcast(F32)
-                for u in range(2):
-                    nc.tensor.transpose(turned[:, s, u, :], pairs[:, u * P:(u + 1) * P], ident[:])
-            hb = work.tile([P, n * PASS], BF16, name="hb", align_bytes=64)
+        def quantise_x(e, lo=0, hi=C):
+            rounded = work.tile([P, (hi - lo) * PACK], BF16, name="x_rounded", align_bytes=64, bufs=X_ROUNDED_BUFS)
             nc.scalar.copy(
-                out=hb[:].bitcast(F32).rearrange("p (s j u) -> p s j u", s=n, u=2),
-                in_=turned[:].rearrange("p s u j -> p s j u"),
+                out=rounded[:].rearrange("p (c two d) -> p c d two", two=2, d=PACK),
+                in_=gathered[e][:, :, lo:hi].rearrange("p d (c two) -> p c d two", two=2),
             )
-            codes, scales = quantise(hb, n * P, "h", 4)
-            return [(codes[:, s * P:(s + 1) * P], scales[:, s * P:(s + 1) * P]) for s in range(n)]
+            for c, operand in enumerate(quantise(rounded[:], hi - lo, "x", X_MX_BUFS)):
+                x_mx[(e * C + lo) // P + c] = operand
 
-        def second_layer(j, h_mx):
-            e = j // 2
-            y = psum.tile([P, P], F32, name="y", bufs=1)
-            for s in range(HP):
-                codes, scales = h_mx[s]
+        def first_product(unit, words, scales, name, banks):
+            j, s = divmod(unit, H_PASSES)
+            e = j // TILES_PER_EXPERT
+            sums = psum.tile([P, PASS], F32, name=name, bufs=banks)
+            nc.tensor.matmul_mx(
+                out=sums[:], lhsT=x_mx[j][0], lhsT_scale=x_mx[j][1],
+                rhs=words[:, e, 2 * PASS * s:2 * PASS * (s + 1)].bitcast(FP4X4),
+                rhs_scale=scales[:, e, PASS * s:PASS * (s + 1)], start=True, stop=True,
+            )
+            return sums[:].rearrange("j (p u v) -> j u p v", u=2, v=2)
+
+        shared_rows = {H_PASSES * d - 1: d for d in range(1, PACK)}
+
+        def activate(unit):
+            sums = first_product(unit, w1_sb, s1_sb, "a", A_BANKS)
+            if unit in shared_rows:
+                act = gathered[E - 1][:, shared_rows[unit], :]
+            else:
+                act = work.tile([P, PASS], F32, name="act", bufs=ACT_BUFS)[:]
+            act_of[unit] = act.rearrange("j (u p v) -> j u p v", u=2, v=2)
+            nc.scalar.activation(out=act_of[unit], in_=sums, func=SILU)
+
+        def multiply(unit):
+            sums = first_product(unit, w3_sb, s3_sb, "b", B_BANKS)
+            h = work.tile([P, PASS], BF16, name="h", bufs=H_BUFS)
+            nc.vector.tensor_tensor(h[:].rearrange("j (u p v) -> j u p v", u=2, v=2), act_of[unit], sums, MULT)
+            h_of[unit] = h[:].bitcast(F32)
+
+        def turn(j):
+            bank = psum.tile([P, H_PASSES, 2, P], F32, name="turn_bank", bufs=TURN_BANKS)
+            for s in range(H_PASSES):
+                for u in range(2):
+                    nc.tensor.transpose(bank[:, s, u, :], h_of[H_PASSES * j + s][:, u * P:(u + 1) * P], identity[:])
+            first, count = (j - j % 2, 2) if j < PAIRED_TILES else (j, 1)
+            if j == first:
+                turned_of[first] = work.tile([P, count, H], BF16, name="h_turned", align_bytes=64, bufs=H_TURNED_BUFS)
+            copy = nc.vector.tensor_copy if j == TURNED_BY_VECTOR else nc.scalar.copy
+            copy(
+                out=turned_of[first][:, j - first, :].bitcast(F32).rearrange("p (s c u) -> p s c u", s=H_PASSES, u=2),
+                in_=bank[:].rearrange("p s u c -> p s c u"),
+            )
+            if j == first + count - 1:
+                values = turned_of[first][:].rearrange("p n i -> p (n i)")
+                for c, operand in enumerate(quantise(values, count * H // PACK, "h", H_MX_BUFS)):
+                    h_mx[H_PASSES * first + c] = operand
+
+        def second_product(j):
+            e, c = divmod(j, TILES_PER_EXPERT)
+            if c == 0:
+                y_bank[e] = psum.tile([P, C], F32, name="y", bufs=Y_BANKS)
+            for s in range(H_PASSES):
+                codes, scales = h_mx[H_PASSES * j + s]
                 nc.tensor.matmul_mx(
-                    out=y[:], lhsT=w2_t[:, e * HP + s, :].bitcast(FP4X4), lhsT_scale=s2_t[:, e * HP + s, :],
-                    rhs=codes.bitcast(FP8X4), rhs_scale=scales, start=(s == 0), stop=(s == HP - 1),
+                    out=y_bank[e][:, c * P:(c + 1) * P],
+                    lhsT=w2_sb[:, e * H_PASSES + s, :].bitcast(FP4X4), lhsT_scale=s2_sb[:, e * H_PASSES + s, :],
+                    rhs=codes, rhs_scale=scales, start=(s == 0), stop=(s == H_PASSES - 1),
                 )
-            nc.scalar.copy(out=y_all[:, j * P:(j + 1) * P], in_=y[:])
+            if c == TILES_PER_EXPERT - 1:
+                nc.scalar.copy(out=y_sb[:, e * C:(e + 1) * C], in_=y_bank[e][:])
 
-        hs, h_mx = {}, {}
-        prepare_tile(0)
-        prepare_tile(1)
-        hs[0] = [first_layer(0, 0)]
-        hs[0].append(first_layer(0, 1))
-        prepare_tile(2)
-        hs[1] = [first_layer(1, 0)]
-        hs[1].append(first_layer(1, 1))
-        h_mx[0] = turn(hs[0])
-        prepare_tile(3)
-        hs[2] = [first_layer(2, 0)]
-        hs[2].append(first_layer(2, 1))
-        h_mx[1] = turn(hs[1])
-        second_layer(0, h_mx[0])
-        prepare_tile(4)
-        hs[3] = [first_layer(3, 0)]
-        hs[3].append(first_layer(3, 1))
-        h_mx[2] = turn(hs[2])
-        second_layer(1, h_mx[1])
-        prepare_tile(5)
-        hs[4] = [first_layer(4, 0)]
-        hs[4].append(first_layer(4, 1))
-        h_mx[3] = turn(hs[3])
-        second_layer(2, h_mx[2])
-        prepare_tile(6)
-        hs[5] = [first_layer(5, 0)]
-        hs[5].append(first_layer(5, 1))
-        h_mx[4] = turn(hs[4])
-        second_layer(3, h_mx[3])
-        prepare_tile(7)
-        hs[6] = [first_layer(6, 0)]
-        hs[6].append(first_layer(6, 1))
-        h_mx[5] = turn(hs[5])
-        second_layer(4, h_mx[4])
-        hs[7] = [first_layer(7, 0)]
-        hs[7].append(first_layer(7, 1))
-        h_mx[6] = turn(hs[6])
-        second_layer(5, h_mx[5])
-        early = turn(hs[7][:1])
-        second_layer(6, h_mx[6])
-        second_layer(7, early + turn(hs[7][1:]))
+        for d in range(PACK - 1):
+            gather(0, d)
+        for lo in range(0, C, P):
+            gather(0, PACK - 1, lo, lo + P)
+            quantise_x(0, lo, lo + P)
+        for d in range(PACK):
+            gather(1, d)
+        quantise_x(1)
+        for d in range(PACK):
+            gather(2, d)
+        gather(E - 1, 0)
+        quantise_x(2)
+
+        for unit in range(ACT_LEAD):
+            activate(unit)
+        for step in range(UNITS + TURN_LAG + SECOND_LAG):
+            if step + ACT_LEAD < UNITS:
+                activate(step + ACT_LEAD)
+            if step < UNITS:
+                multiply(step)
+            if step in shared_rows:
+                gather(E - 1, shared_rows[step])
+                if shared_rows[step] == PACK - 1:
+                    quantise_x(E - 1)
+            if step % H_PASSES == H_PASSES - 1:
+                j_second = (step - TURN_LAG - SECOND_LAG) // H_PASSES
+                j_turn = (step - TURN_LAG) // H_PASSES
+                if j_second >= 0:
+                    second_product(j_second)
+                if 0 <= j_turn < TILES:
+                    turn(j_turn)
 
         half = T // 2
-        for c in range(2):
-            cols = slice(c * half // PER, (c + 1) * half // PER)
-            y1 = work.tile([P, half], F32, name="y1")
-            y2 = work.tile([P, half], F32, name="y2")
-            total = work.tile([P, half], F32, name="total")
-            nc.vector.tensor_copy(y1[:], y_all[:].indirect(pos1_t[:, cols]))
-            nc.vector.tensor_copy(y2[:], y_all[:].indirect(pos2_t[:, cols]))
-            nc.vector.tensor_tensor(total[:], y1[:], y2[:], ADD)
-            nc.sync.dma_start(out=out[:, c * half:(c + 1) * half], in_=total[:])
+        for lo, adder in ((0, nc.gpsimd), (half, nc.vector)):
+            columns = slice(lo // PER_COLUMN, (lo + half) // PER_COLUMN)
+            y1 = work.tile([P, half], F32, name="y1", bufs=RESULT_BUFS)
+            y2 = work.tile([P, half], F32, name="y2", bufs=RESULT_BUFS)
+            total = work.tile([P, half], F32, name="total", bufs=RESULT_BUFS)
+            nc.vector.tensor_copy(y1[:], y_sb[:].indirect(pos1_sb[:, columns]))
+            nc.vector.tensor_copy(y2[:], y_sb[:].indirect(pos2_sb[:, columns]))
+            adder.tensor_tensor(total[:], y1[:], y2[:], ADD)
+            nc.sync.dma_start(out=out[:, lo:lo + half], in_=total[:])

@@ -19,14 +19,7 @@ SCALE_ROWS = 4
 FLOPS = 2 * SLOTS * (2 * K * H + H * N)
 BYTES = 4 * K * T + 4 * P * SLOTS + E * (2 * K * H + H * N) * 17 // 32 + 2 * P * (SLOTS + 2 * T) // PER_COLUMN + 4 * N * T
 
-ACT_LEAD = 2
-TURN_LAG = 2
-SECOND_LAG = 4
-PAIRED_TILES = 4
-TURNED_BY_VECTOR = TILES - 2
-
-A_BANKS, B_BANKS, TURN_BANKS, Y_BANKS = 3, 2, 2, 1
-X_ROUNDED_BUFS, X_MX_BUFS, ACT_BUFS, H_BUFS, H_TURNED_BUFS, H_MX_BUFS, RESULT_BUFS = 3, 2, 6, 12, 4, 6, 2
+ROUNDS = ((0, 3 * P), (3 * P, 3 * P), (6 * P, 2 * P))
 
 F32 = mybir.dt.float32
 BF16 = mybir.dt.bfloat16
@@ -61,14 +54,21 @@ def tile_moe_pre_glu_silu_kernel(
         s1_sb = keep.tile([P, E, H], U8, name="s1_sb", align_bytes=64)
         s3_sb = keep.tile([P, E, H], U8, name="s3_sb", align_bytes=64)
         s2_sb = keep.tile([P, E * H_PASSES, N], U8, name="s2_sb", align_bytes=64)
-        gathered = [keep.tile([P, PACK, PASS], F32, name="gathered%d" % e) for e in range(E)]
+        width = 3 * P
+        early = keep.tile([P, PACK * width + 2 * P], F32, name="early")
+        late = keep.tile([P, PACK, PASS], F32, name="late")
+        gathered = [
+            early[:, 2 * P:].rearrange("p (d c) -> p d c", d=PACK),
+            early[:, :PACK * width].rearrange("p (d c) -> p d c", d=PACK),
+            late[:],
+        ]
         identity = keep.tile([P, P], F32, name="identity")
         y_sb = keep.tile([P, SLOTS], F32, name="y_sb")
         warm = keep.tile([P, 2], F32, name="warm")
 
         def load_words(tile, words, lo, hi):
             by_pass = words.rearrange("e s p n -> p (e s) n")
-            nc.sync.dma_start(out=tile[:, lo:hi, :].bitcast(I32), in_=by_pass[:, lo:hi, :].bitcast(I32))
+            nc.sync.dma_start(out=tile.bitcast(I32), in_=by_pass[:, lo:hi, :].bitcast(I32))
 
         def load_scales(tile, scales):
             rows = scales.rearrange("e s (q r) n -> r q (e s) n", r=SCALE_ROWS)
@@ -84,148 +84,189 @@ def tile_moe_pre_glu_silu_kernel(
         nc.scalar.activation(out=warm[:, 1:2], in_=warm[:, 0:1], func=SILU)
 
         x_by_d = xT.rearrange("(p d) t -> d p t", d=PACK)
-        nc.sync.dma_start(offs_sb[:], offs)
         nc.sync.dma_start(out=x_rows[0][:], in_=x_by_d[0])
-        load_gate(0, C)
+        nc.sync.dma_start(offs_sb[:], offs)
+        load_gate(0, 3 * P)
         for d in range(1, PACK):
             nc.sync.dma_start(out=x_rows[d][:], in_=x_by_d[d])
-        load_gate(C, 2 * C)
-        load_words(w1_sb, w1_words, 0, 1)
+        load_gate(3 * P, 6 * P)
+        load_words(w1_sb[:, 0:1, :], w1_words, 0, 1)
         load_scales(s1_sb, w1_scales)
-        load_gate(2 * C, SLOTS)
-        load_words(w3_sb, w3_words, 0, 1)
+        load_words(w1_sb[:, 1:2, :], w1_words, 1, 2)
+        load_words(w3_sb[:, 0:1, :], w3_words, 0, 1)
         load_scales(s3_sb, w3_scales)
-        load_words(w1_sb, w1_words, 1, 2)
-        load_words(w3_sb, w3_words, 1, 2)
-        load_words(w2_sb, w2_words, 0, E * H_PASSES)
+        load_words(w3_sb[:, 1:2, :], w3_words, 1, 2)
+        load_gate(6 * P, SLOTS)
+        load_words(w1_sb[:, 2:E, :], w1_words, 2, E)
+        load_words(w3_sb[:, 2:E, :], w3_words, 2, E)
+        load_words(w2_sb[:], w2_words, 0, E * H_PASSES)
         load_scales(s2_sb, w2_scales)
-        load_words(w1_sb, w1_words, 2, E)
-        load_words(w3_sb, w3_words, 2, E)
         nc.sync.dma_start(pos1_sb[:], pos1)
         nc.sync.dma_start(pos2_sb[:], pos2)
         make_identity(nc, identity[:])
 
-        x_mx, act_of, h_of, turned_of, h_mx, y_bank = {}, {}, {}, {}, {}, {}
+        x_tiles = {}
+        x_mx, rounded_of, act_of, b_of, h_of, turned_of, h_mx = {}, {}, {}, {}, {}, {}, {}
 
-        def quantise(values, width, name, bufs):
-            codes = work.tile([P, width], U32, name=name + "_codes", align_bytes=64, bufs=bufs)
-            scales = work.tile([P, width], U8, name=name + "_scales", align_bytes=64, bufs=bufs)
-            nc.vector.quantize_mx(out=codes[:].bitcast(FP8X4), scales=scales[:], in_=values)
-            return [(codes[:, c:c + P].bitcast(FP8X4), scales[:, c:c + P]) for c in range(0, width, P)]
+        def mx_tiles(width, name, tag=None):
+            codes = work.tile([P, width], U32, name=name + "_codes", tag=tag or name + "_codes", align_bytes=64)
+            scales = work.tile([P, width], U8, name=name + "_scales", align_bytes=64)
+            return codes, scales
 
-        def gather(e, d, lo=0, hi=C):
-            first, end = e * C + lo, e * C + hi
+        def quantise(values, codes, scales, lo, hi):
+            nc.vector.quantize_mx(out=codes[:, lo:hi].bitcast(FP8X4), scales=scales[:, lo:hi], in_=values)
+            return [(codes[:, c:c + P].bitcast(FP8X4), scales[:, c:c + P]) for c in range(lo, hi, P)]
+
+        def gather(r, d, lo=0, hi=None):
+            base, width = ROUNDS[r]
+            first, end = base + lo, base + (hi or width)
             tokens = x_rows[d][:].indirect(offs_sb[:, first // PER_COLUMN:end // PER_COLUMN])
-            nc.vector.tensor_tensor(gathered[e][:, d, lo:hi], tokens, gate_sb[:, first:end], MULT)
+            nc.vector.tensor_tensor(gathered[r][:, d, first - base:end - base], tokens, gate_sb[:, first:end], MULT)
 
-        def quantise_x(e, lo=0, hi=C):
-            rounded = work.tile([P, (hi - lo) * PACK], BF16, name="x_rounded", align_bytes=64, bufs=X_ROUNDED_BUFS)
+        def round_x(r, lo, hi, tag=None):
+            if lo == 0:
+                name = "x_rounded%d" % r
+                rounded_of[r] = work.tile([P, ROUNDS[r][1] * PACK], BF16, name=name, tag=tag or name, align_bytes=64)
+            rounded_of[r, lo] = rounded_of[r][:, lo * PACK:hi * PACK]
             nc.scalar.copy(
-                out=rounded[:].rearrange("p (c two d) -> p c d two", two=2, d=PACK),
-                in_=gathered[e][:, :, lo:hi].rearrange("p d (c two) -> p c d two", two=2),
+                out=rounded_of[r, lo].rearrange("p (c two d) -> p c d two", two=2, d=PACK),
+                in_=gathered[r][:, :, lo:hi].rearrange("p d (c two) -> p c d two", two=2),
             )
-            for c, operand in enumerate(quantise(rounded[:], hi - lo, "x", X_MX_BUFS)):
-                x_mx[(e * C + lo) // P + c] = operand
 
-        def first_product(unit, words, scales, name, banks):
+        def quantise_x(r, lo, hi, tag=None):
+            if lo == 0:
+                x_tiles[r] = mx_tiles(ROUNDS[r][1], "x%d" % r, tag)
+            for c, operand in enumerate(quantise(rounded_of[r, lo], *x_tiles[r], lo, hi)):
+                x_mx[(ROUNDS[r][0] + lo) // P + c] = operand
+
+        def first_product(unit, words, scales, bank):
             j, s = divmod(unit, H_PASSES)
             e = j // TILES_PER_EXPERT
-            sums = psum.tile([P, PASS], F32, name=name, bufs=banks)
+            sums = psum.tile([P, PASS], F32, name="sums", tag=bank)
             nc.tensor.matmul_mx(
                 out=sums[:], lhsT=x_mx[j][0], lhsT_scale=x_mx[j][1],
-                rhs=words[:, e, 2 * PASS * s:2 * PASS * (s + 1)].bitcast(FP4X4),
+                rhs=words[:, 2 * PASS * s:2 * PASS * (s + 1)].bitcast(FP4X4),
                 rhs_scale=scales[:, e, PASS * s:PASS * (s + 1)], start=True, stop=True,
             )
             return sums[:].rearrange("j (p u v) -> j u p v", u=2, v=2)
 
-        shared_rows = {H_PASSES * d - 1: d for d in range(1, PACK)}
+        shared_rows = {2 + d: gathered[2][:, d, :] for d in range(PACK)}
 
         def activate(unit):
-            sums = first_product(unit, w1_sb, s1_sb, "a", A_BANKS)
+            e = unit // (H_PASSES * TILES_PER_EXPERT)
+            sums = first_product(unit, w1_sb[:, e, :], s1_sb, "a%d" % (unit % 3))
             if unit in shared_rows:
-                act = gathered[E - 1][:, shared_rows[unit], :]
+                act = shared_rows[unit]
             else:
-                act = work.tile([P, PASS], F32, name="act", bufs=ACT_BUFS)[:]
+                act = work.tile([P, PASS], F32, name="act", tag="act%d" % unit, align_bytes=64)[:]
             act_of[unit] = act.rearrange("j (u p v) -> j u p v", u=2, v=2)
             nc.scalar.activation(out=act_of[unit], in_=sums, func=SILU)
 
+        def linear(unit):
+            if unit < UNITS:
+                e = unit // (H_PASSES * TILES_PER_EXPERT)
+                b_of[unit] = first_product(unit, w3_sb[:, e, :], s3_sb, "b%d" % (unit % 3))
+
         def multiply(unit):
-            sums = first_product(unit, w3_sb, s3_sb, "b", B_BANKS)
-            h = work.tile([P, PASS], BF16, name="h", bufs=H_BUFS)
-            nc.vector.tensor_tensor(h[:].rearrange("j (u p v) -> j u p v", u=2, v=2), act_of[unit], sums, MULT)
+            h = work.tile([P, PASS], BF16, name="h", tag="h%d" % unit)
+            nc.vector.tensor_tensor(h[:].rearrange("j (u p v) -> j u p v", u=2, v=2), act_of[unit], b_of[unit], MULT)
             h_of[unit] = h[:].bitcast(F32)
 
-        def turn(j):
-            bank = psum.tile([P, H_PASSES, 2, P], F32, name="turn_bank", bufs=TURN_BANKS)
-            for s in range(H_PASSES):
+        groups = [(0, 4), (4, 4), (8, 2), (10, 2), (12, 2), (14, 1), (15, 1)]
+        group_of = {u: g for g in groups for u in range(g[0], g[0] + g[1])}
+
+        def turn(unit, count, bank_tag):
+            bank = psum.tile([P, count, 2, P], F32, name="turn_bank", tag=bank_tag)
+            for s in range(count):
                 for u in range(2):
-                    nc.tensor.transpose(bank[:, s, u, :], h_of[H_PASSES * j + s][:, u * P:(u + 1) * P], identity[:])
-            first, count = (j - j % 2, 2) if j < PAIRED_TILES else (j, 1)
-            if j == first:
-                turned_of[first] = work.tile([P, count, H], BF16, name="h_turned", align_bytes=64, bufs=H_TURNED_BUFS)
-            copy = nc.vector.tensor_copy if j == TURNED_BY_VECTOR else nc.scalar.copy
-            copy(
-                out=turned_of[first][:, j - first, :].bitcast(F32).rearrange("p (s c u) -> p s c u", s=H_PASSES, u=2),
+                    nc.tensor.transpose(bank[:, s, u, :], h_of[unit + s][:, u * P:(u + 1) * P], identity[:])
+            first, units = group_of[unit]
+            if unit == first:
+                turned_of[first] = work.tile([P, units * PASS], BF16, name="h_turned", tag="h_turned%d" % first, align_bytes=64)
+            lo = (unit - first) * PASS
+            nc.scalar.copy(
+                out=turned_of[first][:, lo:lo + count * PASS].bitcast(F32).rearrange("p (s c u) -> p s c u", s=count, u=2),
                 in_=bank[:].rearrange("p s u c -> p s c u"),
             )
-            if j == first + count - 1:
-                values = turned_of[first][:].rearrange("p n i -> p (n i)")
-                for c, operand in enumerate(quantise(values, count * H // PACK, "h", H_MX_BUFS)):
-                    h_mx[H_PASSES * first + c] = operand
 
-        def second_product(j):
-            e, c = divmod(j, TILES_PER_EXPERT)
-            if c == 0:
-                y_bank[e] = psum.tile([P, C], F32, name="y", bufs=Y_BANKS)
-            for s in range(H_PASSES):
-                codes, scales = h_mx[H_PASSES * j + s]
-                nc.tensor.matmul_mx(
-                    out=y_bank[e][:, c * P:(c + 1) * P],
-                    lhsT=w2_sb[:, e * H_PASSES + s, :].bitcast(FP4X4), lhsT_scale=s2_sb[:, e * H_PASSES + s, :],
-                    rhs=codes, rhs_scale=scales, start=(s == 0), stop=(s == H_PASSES - 1),
-                )
-            if c == TILES_PER_EXPERT - 1:
-                nc.scalar.copy(out=y_sb[:, e * C:(e + 1) * C], in_=y_bank[e][:])
+        def quantise_h(first, tag=None):
+            units = group_of[first][1]
+            for c, operand in enumerate(quantise(turned_of[first][:], *mx_tiles(units * P, "h%d" % first, tag), 0, units * P)):
+                h_mx[first + c] = operand
+
+        def second_product(first, count, bank_tag):
+            bank = psum.tile([P, count * P], F32, name="y", tag=bank_tag)
+            for c in range(count):
+                j = first + c
+                e = j // TILES_PER_EXPERT
+                for s in range(H_PASSES):
+                    codes, scales = h_mx[H_PASSES * j + s]
+                    nc.tensor.matmul_mx(
+                        out=bank[:, c * P:(c + 1) * P],
+                        lhsT=w2_sb[:, e * H_PASSES + s, :].bitcast(FP4X4), lhsT_scale=s2_sb[:, e * H_PASSES + s, :],
+                        rhs=codes, rhs_scale=scales, start=(s == 0), stop=(s == H_PASSES - 1),
+                    )
+            nc.scalar.copy(out=y_sb[:, first * P:(first + count) * P], in_=bank[:])
 
         for d in range(PACK - 1):
             gather(0, d)
-        for lo in range(0, C, P):
-            gather(0, PACK - 1, lo, lo + P)
-            quantise_x(0, lo, lo + P)
+        for lo, hi in ((0, P), (P, 3 * P)):
+            gather(0, PACK - 1, lo, hi)
+            round_x(0, lo, hi)
+            quantise_x(0, lo, hi)
         for d in range(PACK):
             gather(1, d)
-        quantise_x(1)
-        for d in range(PACK):
-            gather(2, d)
-        gather(E - 1, 0)
-        quantise_x(2)
-
-        for unit in range(ACT_LEAD):
+        for unit in range(6):
             activate(unit)
-        for step in range(UNITS + TURN_LAG + SECOND_LAG):
-            if step + ACT_LEAD < UNITS:
-                activate(step + ACT_LEAD)
-            if step < UNITS:
-                multiply(step)
-            if step in shared_rows:
-                gather(E - 1, shared_rows[step])
-                if shared_rows[step] == PACK - 1:
-                    quantise_x(E - 1)
-            if step % H_PASSES == H_PASSES - 1:
-                j_second = (step - TURN_LAG - SECOND_LAG) // H_PASSES
-                j_turn = (step - TURN_LAG) // H_PASSES
-                if j_second >= 0:
-                    second_product(j_second)
-                if 0 <= j_turn < TILES:
-                    turn(j_turn)
+        for unit in range(3):
+            linear(unit)
 
-        half = T // 2
-        for lo, adder in ((0, nc.gpsimd), (half, nc.vector)):
-            columns = slice(lo // PER_COLUMN, (lo + half) // PER_COLUMN)
-            y1 = work.tile([P, half], F32, name="y1", bufs=RESULT_BUFS)
-            y2 = work.tile([P, half], F32, name="y2", bufs=RESULT_BUFS)
-            total = work.tile([P, half], F32, name="total", bufs=RESULT_BUFS)
-            nc.vector.tensor_copy(y1[:], y_sb[:].indirect(pos1_sb[:, columns]))
-            nc.vector.tensor_copy(y2[:], y_sb[:].indirect(pos2_sb[:, columns]))
-            adder.tensor_tensor(total[:], y1[:], y2[:], ADD)
-            nc.sync.dma_start(out=out[:, lo:lo + half], in_=total[:])
+        def after_product(unit):
+            if unit == 0:
+                round_x(1, 0, P, tag="act0")
+                round_x(1, P, 3 * P)
+            if unit == 2:
+                quantise_x(1, 0, P, tag="act1")
+            if 3 <= unit <= 6:
+                gather(2, unit - 3)
+            if unit == 3:
+                quantise_x(1, P, 3 * P)
+            if unit == 6:
+                round_x(2, 0, 2 * P)
+            if unit == 7:
+                quantise_h(0)
+            if unit == 8:
+                quantise_x(2, 0, 2 * P, tag="act7")
+            if unit == 11:
+                quantise_h(4)
+
+        for unit in range(UNITS):
+            multiply(unit)
+            after_product(unit)
+            linear(unit + 3)
+            if 2 <= unit < UNITS - 4:
+                activate(unit + 4)
+            if unit >= UNITS - 2:
+                turn(unit, 1, "t1" if unit % 2 == 0 else "b2")
+            elif unit % 2 == 1:
+                turn(unit - 1, 2, "t%d" % (unit // 2 % 2))
+            if unit == 11:
+                second_product(0, 4, "a1")
+        quantise_h(8, tag="act14")
+        quantise_h(10, tag="act13")
+        second_product(4, 2, "a2")
+        quantise_h(12)
+        second_product(6, 1, "a0")
+        quantise_h(14)
+        quantise_h(15)
+        second_product(7, 1, "b1")
+
+        pieces = ((0, 3 * P), (3 * P, T))
+        columns = [slice(lo // PER_COLUMN, hi // PER_COLUMN) for lo, hi in pieces]
+        y1 = [work.tile([P, hi - lo], F32, name="y1_%d" % lo) for lo, hi in pieces]
+        total = [work.tile([P, hi - lo], F32, name="total%d" % lo) for lo, hi in pieces]
+        for c in range(2):
+            nc.vector.tensor_copy(y1[c][:], y_sb[:].indirect(pos1_sb[:, columns[c]]))
+        for c in range(2):
+            nc.vector.tensor_tensor(total[c][:], y_sb[:].indirect(pos2_sb[:, columns[c]]), y1[c][:], ADD)
+            nc.sync.dma_start(out=out[:, pieces[c][0]:pieces[c][1]], in_=total[c][:])

@@ -194,7 +194,7 @@ def tile_moe_pre_glu_silu_kernel(
             for c, operand in enumerate(quantise(turned_of[first][:], *mx_tiles(units * P, "h%d" % first, tag), 0, units * P)):
                 h_mx[first + c] = operand
 
-        def second_product(first, count, bank_tag):
+        def second_product(first, count, bank_tag, copy=nc.scalar.copy):
             bank = psum.tile([P, count * P], F32, name="y", tag=bank_tag)
             for c in range(count):
                 j = first + c
@@ -206,7 +206,7 @@ def tile_moe_pre_glu_silu_kernel(
                         lhsT=w2_sb[:, e * H_PASSES + s, :].bitcast(FP4X4), lhsT_scale=s2_sb[:, e * H_PASSES + s, :],
                         rhs=codes, rhs_scale=scales, start=(s == 0), stop=(s == H_PASSES - 1),
                     )
-            nc.scalar.copy(out=y_sb[:, first * P:(first + count) * P], in_=bank[:])
+            return lambda: copy(out=y_sb[:, first * P:(first + count) * P], in_=bank[:])
 
         for d in range(PACK - 1):
             gather(0, d)
@@ -250,16 +250,16 @@ def tile_moe_pre_glu_silu_kernel(
                 turn(unit, 1, "t1" if unit % 2 == 0 else "b2")
             elif unit % 2 == 1:
                 turn(unit - 1, 2, "t%d" % (unit // 2 % 2))
-            if unit == 11:
-                second_product(0, 4, "a1")
+        empty_first = second_product(0, 4, "b0", nc.vector.tensor_copy)
         quantise_h(8, tag="act14")
         quantise_h(10, tag="act13")
-        second_product(4, 2, "a2")
+        second_product(4, 2, "a2")()
         quantise_h(12)
-        second_product(6, 1, "a0")
+        second_product(6, 1, "a0")()
         quantise_h(14)
         quantise_h(15)
-        second_product(7, 1, "b1")
+        second_product(7, 1, "b1")()
+        empty_first()
 
         pieces = ((0, 3 * P), (3 * P, T))
         columns = [slice(lo // PER_COLUMN, hi // PER_COLUMN) for lo, hi in pieces]

@@ -19,7 +19,8 @@ SCALE_ROWS = 4
 FLOPS = 2 * SLOTS * (2 * K * H + H * N)
 BYTES = 4 * K * T + 4 * P * SLOTS + E * (2 * K * H + H * N) * 17 // 32 + 2 * P * (SLOTS + 2 * T) // PER_COLUMN + 4 * N * T
 
-ROUNDS = ((0, 3 * P), (3 * P, 3 * P), (6 * P, 2 * P))
+VECTOR_SLOTS = 3 * P
+SCALAR_PIECES = ((VECTOR_SLOTS, 4 * P + 32), (4 * P + 32, SLOTS))
 
 F32 = mybir.dt.float32
 BF16 = mybir.dt.bfloat16
@@ -32,6 +33,7 @@ FP4X4 = mybir.dt.float4_e2m1fn_x4
 MULT = mybir.AluOpType.mult
 ADD = mybir.AluOpType.add
 SILU = mybir.ActivationFunctionType.Silu
+COPY = mybir.ActivationFunctionType.Copy
 
 
 def tile_moe_pre_glu_silu_kernel(
@@ -54,14 +56,9 @@ def tile_moe_pre_glu_silu_kernel(
         s1_sb = keep.tile([P, E, H], U8, name="s1_sb", align_bytes=64)
         s3_sb = keep.tile([P, E, H], U8, name="s3_sb", align_bytes=64)
         s2_sb = keep.tile([P, E * H_PASSES, N], U8, name="s2_sb", align_bytes=64)
-        width = 3 * P
-        early = keep.tile([P, PACK * width + 2 * P], F32, name="early")
-        late = keep.tile([P, PACK, PASS], F32, name="late")
-        gathered = [
-            early[:, 2 * P:].rearrange("p (d c) -> p d c", d=PACK),
-            early[:, :PACK * width].rearrange("p (d c) -> p d c", d=PACK),
-            late[:],
-        ]
+        weighted = keep.tile([P, PACK, VECTOR_SLOTS], F32, name="weighted")
+        plain = [keep.tile([P, PACK, hi - lo], F32, name="plain%d" % lo) for lo, hi in SCALAR_PIECES]
+        x_bf16 = keep.tile([P, SLOTS * PACK], BF16, name="x_bf16", align_bytes=64)
         identity = keep.tile([P, P], F32, name="identity")
         y_sb = keep.tile([P, SLOTS], F32, name="y_sb")
         warm = keep.tile([P, 2], F32, name="warm")
@@ -86,17 +83,16 @@ def tile_moe_pre_glu_silu_kernel(
         x_by_d = xT.rearrange("(p d) t -> d p t", d=PACK)
         nc.sync.dma_start(out=x_rows[0][:], in_=x_by_d[0])
         nc.sync.dma_start(offs_sb[:], offs)
-        load_gate(0, 3 * P)
+        load_gate(0, VECTOR_SLOTS)
         for d in range(1, PACK):
             nc.sync.dma_start(out=x_rows[d][:], in_=x_by_d[d])
-        load_gate(3 * P, 6 * P)
         load_words(w1_sb[:, 0:1, :], w1_words, 0, 1)
         load_scales(s1_sb, w1_scales)
-        load_words(w1_sb[:, 1:2, :], w1_words, 1, 2)
+        load_gate(VECTOR_SLOTS, SLOTS)
         load_words(w3_sb[:, 0:1, :], w3_words, 0, 1)
         load_scales(s3_sb, w3_scales)
+        load_words(w1_sb[:, 1:2, :], w1_words, 1, 2)
         load_words(w3_sb[:, 1:2, :], w3_words, 1, 2)
-        load_gate(6 * P, SLOTS)
         load_words(w1_sb[:, 2:E, :], w1_words, 2, E)
         load_words(w3_sb[:, 2:E, :], w3_words, 2, E)
         load_words(w2_sb[:], w2_words, 0, E * H_PASSES)
@@ -105,39 +101,44 @@ def tile_moe_pre_glu_silu_kernel(
         nc.sync.dma_start(pos2_sb[:], pos2)
         make_identity(nc, identity[:])
 
-        x_tiles = {}
-        x_mx, rounded_of, act_of, b_of, h_of, turned_of, h_mx = {}, {}, {}, {}, {}, {}, {}
+        x_mx, act_of, b_of, h_of, turned_of, h_mx = {}, {}, {}, {}, {}, {}
 
-        def mx_tiles(width, name, tag=None):
+        def quantise(values, width, name, tag=None):
             codes = work.tile([P, width], U32, name=name + "_codes", tag=tag or name + "_codes", align_bytes=64)
             scales = work.tile([P, width], U8, name=name + "_scales", align_bytes=64)
-            return codes, scales
+            nc.vector.quantize_mx(out=codes[:].bitcast(FP8X4), scales=scales[:], in_=values)
+            return [(codes[:, c:c + P].bitcast(FP8X4), scales[:, c:c + P]) for c in range(0, width, P)]
 
-        def quantise(values, codes, scales, lo, hi):
-            nc.vector.quantize_mx(out=codes[:, lo:hi].bitcast(FP8X4), scales=scales[:, lo:hi], in_=values)
-            return [(codes[:, c:c + P].bitcast(FP8X4), scales[:, c:c + P]) for c in range(lo, hi, P)]
+        def tokens(d, lo, hi):
+            return x_rows[d][:].indirect(offs_sb[:, lo // PER_COLUMN:hi // PER_COLUMN])
 
-        def gather(r, d, lo=0, hi=None):
-            base, width = ROUNDS[r]
-            first, end = base + lo, base + (hi or width)
-            tokens = x_rows[d][:].indirect(offs_sb[:, first // PER_COLUMN:end // PER_COLUMN])
-            nc.vector.tensor_tensor(gathered[r][:, d, first - base:end - base], tokens, gate_sb[:, first:end], MULT)
+        def gather_weighted(d, lo, hi):
+            nc.vector.tensor_tensor(weighted[:, d, lo:hi], tokens(d, lo, hi), gate_sb[:, lo:hi], MULT)
 
-        def round_x(r, lo, hi, tag=None):
-            if lo == 0:
-                name = "x_rounded%d" % r
-                rounded_of[r] = work.tile([P, ROUNDS[r][1] * PACK], BF16, name=name, tag=tag or name, align_bytes=64)
-            rounded_of[r, lo] = rounded_of[r][:, lo * PACK:hi * PACK]
-            nc.scalar.copy(
-                out=rounded_of[r, lo].rearrange("p (c two d) -> p c d two", two=2, d=PACK),
-                in_=gathered[r][:, :, lo:hi].rearrange("p d (c two) -> p c d two", two=2),
+        def gather_plain(piece, d):
+            nc.scalar.activation(plain[piece][:, d, :], tokens(d, *SCALAR_PIECES[piece]), COPY)
+
+        def interleaved(lo, hi):
+            return x_bf16[:, lo * PACK:hi * PACK].rearrange("p (c two d) -> p c d two", two=2, d=PACK)
+
+        def by_pairs(rows):
+            return rows.rearrange("p d (c two) -> p c d two", two=2)
+
+        def round_x(lo, hi):
+            nc.vector.tensor_copy(out=interleaved(lo, hi), in_=by_pairs(weighted[:, :, lo:hi]))
+
+        def weigh_and_round(piece, lo, hi):
+            base = SCALAR_PIECES[piece][0]
+            weights = gate_sb[:, lo:hi].rearrange("p (c two) -> p c two", two=2).unsqueeze(2)
+            nc.vector.tensor_tensor(
+                interleaved(lo, hi), by_pairs(plain[piece][:, :, lo - base:hi - base]),
+                weights.to_broadcast([P, (hi - lo) // 2, PACK, 2]), MULT,
             )
 
-        def quantise_x(r, lo, hi, tag=None):
-            if lo == 0:
-                x_tiles[r] = mx_tiles(ROUNDS[r][1], "x%d" % r, tag)
-            for c, operand in enumerate(quantise(rounded_of[r, lo], *x_tiles[r], lo, hi)):
-                x_mx[(ROUNDS[r][0] + lo) // P + c] = operand
+        def quantise_x(first, count):
+            values = x_bf16[:, first * PASS:(first + count) * PASS]
+            for c, operand in enumerate(quantise(values, count * P, "x%d" % first)):
+                x_mx[first + c] = operand
 
         def first_product(unit, words, scales, bank):
             j, s = divmod(unit, H_PASSES)
@@ -145,34 +146,26 @@ def tile_moe_pre_glu_silu_kernel(
             sums = psum.tile([P, PASS], F32, name="sums", tag=bank)
             nc.tensor.matmul_mx(
                 out=sums[:], lhsT=x_mx[j][0], lhsT_scale=x_mx[j][1],
-                rhs=words[:, 2 * PASS * s:2 * PASS * (s + 1)].bitcast(FP4X4),
+                rhs=words[:, e, 2 * PASS * s:2 * PASS * (s + 1)].bitcast(FP4X4),
                 rhs_scale=scales[:, e, PASS * s:PASS * (s + 1)], start=True, stop=True,
             )
             return sums[:].rearrange("j (p u v) -> j u p v", u=2, v=2)
 
-        shared_rows = {2 + d: gathered[2][:, d, :] for d in range(PACK)}
-
         def activate(unit):
-            e = unit // (H_PASSES * TILES_PER_EXPERT)
-            sums = first_product(unit, w1_sb[:, e, :], s1_sb, "a%d" % (unit % 3))
-            if unit in shared_rows:
-                act = shared_rows[unit]
-            else:
-                act = work.tile([P, PASS], F32, name="act", tag="act%d" % unit, align_bytes=64)[:]
-            act_of[unit] = act.rearrange("j (u p v) -> j u p v", u=2, v=2)
+            sums = first_product(unit, w1_sb, s1_sb, "a%d" % (unit % 3))
+            act = work.tile([P, PASS], F32, name="act", tag="act%d" % unit, align_bytes=64)
+            act_of[unit] = act[:].rearrange("j (u p v) -> j u p v", u=2, v=2)
             nc.scalar.activation(out=act_of[unit], in_=sums, func=SILU)
 
         def linear(unit):
-            if unit < UNITS:
-                e = unit // (H_PASSES * TILES_PER_EXPERT)
-                b_of[unit] = first_product(unit, w3_sb[:, e, :], s3_sb, "b%d" % (unit % 3))
+            b_of[unit] = first_product(unit, w3_sb, s3_sb, "b%d" % (unit % 3))
 
         def multiply(unit):
             h = work.tile([P, PASS], BF16, name="h", tag="h%d" % unit)
             nc.vector.tensor_tensor(h[:].rearrange("j (u p v) -> j u p v", u=2, v=2), act_of[unit], b_of[unit], MULT)
             h_of[unit] = h[:].bitcast(F32)
 
-        groups = [(0, 4), (4, 4), (8, 2), (10, 2), (12, 2), (14, 1), (15, 1)]
+        groups = [(0, 4), (4, 4), (8, 4), (12, 2), (14, 1), (15, 1)]
         group_of = {u: g for g in groups for u in range(g[0], g[0] + g[1])}
 
         def turn(unit, count, bank_tag):
@@ -191,7 +184,7 @@ def tile_moe_pre_glu_silu_kernel(
 
         def quantise_h(first, tag=None):
             units = group_of[first][1]
-            for c, operand in enumerate(quantise(turned_of[first][:], *mx_tiles(units * P, "h%d" % first, tag), 0, units * P)):
+            for c, operand in enumerate(quantise(turned_of[first][:], units * P, "h%d" % first, tag)):
                 h_mx[first + c] = operand
 
         def second_product(first, count, bank_tag, copy=nc.scalar.copy):
@@ -206,67 +199,59 @@ def tile_moe_pre_glu_silu_kernel(
                         lhsT=w2_sb[:, e * H_PASSES + s, :].bitcast(FP4X4), lhsT_scale=s2_sb[:, e * H_PASSES + s, :],
                         rhs=codes, rhs_scale=scales, start=(s == 0), stop=(s == H_PASSES - 1),
                     )
-            return lambda: copy(out=y_sb[:, first * P:(first + count) * P], in_=bank[:])
+            copy(out=y_sb[:, first * P:(first + count) * P], in_=bank[:])
 
-        for d in range(PACK - 1):
-            gather(0, d)
-        for lo, hi in ((0, P), (P, 3 * P)):
-            gather(0, PACK - 1, lo, hi)
-            round_x(0, lo, hi)
-            quantise_x(0, lo, hi)
         for d in range(PACK):
-            gather(1, d)
-        for unit in range(6):
+            for piece in range(2):
+                gather_plain(piece, d)
+        for d in range(PACK - 1):
+            gather_weighted(d, 0, VECTOR_SLOTS)
+        for lo, hi in ((0, P), (P, VECTOR_SLOTS)):
+            gather_weighted(PACK - 1, lo, hi)
+        for lo, hi in ((0, P), (P, VECTOR_SLOTS)):
+            round_x(lo, hi)
+        quantise_x(0, 1)
+        quantise_x(1, 2)
+        weigh_and_round(0, *SCALAR_PIECES[0])
+        quantise_x(3, 1)
+        weigh_and_round(1, *SCALAR_PIECES[1])
+        lead = 8
+        for unit in range(lead):
             activate(unit)
-        for unit in range(3):
-            linear(unit)
-
-        def after_product(unit):
-            if unit == 0:
-                round_x(1, 0, P, tag="act0")
-                round_x(1, P, 3 * P)
-            if unit == 2:
-                quantise_x(1, 0, P, tag="act1")
-            if 3 <= unit <= 6:
-                gather(2, unit - 3)
-            if unit == 3:
-                quantise_x(1, P, 3 * P)
-            if unit == 6:
-                round_x(2, 0, 2 * P)
-            if unit == 7:
-                quantise_h(0)
-            if unit == 8:
-                quantise_x(2, 0, 2 * P, tag="act7")
-            if unit == 11:
-                quantise_h(4)
+            if 3 <= unit < 6:
+                linear(unit - 3)
 
         for unit in range(UNITS):
             multiply(unit)
-            after_product(unit)
-            linear(unit + 3)
-            if 2 <= unit < UNITS - 4:
-                activate(unit + 4)
+            if unit == 0:
+                quantise_x(4, 4)
+            if unit in (7, 11):
+                quantise_h(unit - 7)
+            if unit + 3 < UNITS:
+                linear(unit + 3)
             if unit >= UNITS - 2:
-                turn(unit, 1, "t1" if unit % 2 == 0 else "b2")
+                turn(unit, 1, "t%d" % (unit % 2))
             elif unit % 2 == 1:
                 turn(unit - 1, 2, "t%d" % (unit // 2 % 2))
-        empty_first = second_product(0, 4, "b0", nc.vector.tensor_copy)
+                for ahead in range(unit + lead - 1, min(unit + lead + 1, UNITS)):
+                    activate(ahead)
         quantise_h(8, tag="act14")
-        quantise_h(10, tag="act13")
-        second_product(4, 2, "a2")()
+        second_product(0, 4, "a1")
         quantise_h(12)
-        second_product(6, 1, "a0")()
+        second_product(4, 3, "a2")
         quantise_h(14)
         quantise_h(15)
-        second_product(7, 1, "b1")()
-        empty_first()
+        second_product(7, 1, "a0")
 
-        pieces = ((0, 3 * P), (3 * P, T))
+        pieces = ((0, P), (P, 2 * P), (2 * P, T))
         columns = [slice(lo // PER_COLUMN, hi // PER_COLUMN) for lo, hi in pieces]
         y1 = [work.tile([P, hi - lo], F32, name="y1_%d" % lo) for lo, hi in pieces]
-        total = [work.tile([P, hi - lo], F32, name="total%d" % lo) for lo, hi in pieces]
-        for c in range(2):
-            nc.vector.tensor_copy(y1[c][:], y_sb[:].indirect(pos1_sb[:, columns[c]]))
-        for c in range(2):
-            nc.vector.tensor_tensor(total[c][:], y_sb[:].indirect(pos2_sb[:, columns[c]]), y1[c][:], ADD)
-            nc.sync.dma_start(out=out[:, pieces[c][0]:pieces[c][1]], in_=total[c][:])
+        total = [work.tile([P, 2 * P], F32, name="total%d" % half) for half in range(2)]
+        nc.vector.tensor_copy(y1[1][:], y_sb[:].indirect(pos1_sb[:, columns[1]]))
+        for c in (0, 2):
+            nc.scalar.activation(y1[c][:], y_sb[:].indirect(pos1_sb[:, columns[c]]), COPY)
+        for c, (lo, hi) in enumerate(pieces):
+            half, first = divmod(lo, 2 * P)
+            nc.vector.tensor_tensor(total[half][:, first:first + hi - lo], y_sb[:].indirect(pos2_sb[:, columns[c]]), y1[c][:], ADD)
+            if c > 0:
+                nc.sync.dma_start(out=out[:, 2 * P * half:2 * P * (half + 1)], in_=total[half][:])

@@ -19,8 +19,8 @@ SCALE_ROWS = 4
 FLOPS = 2 * SLOTS * (2 * K * H + H * N)
 BYTES = 4 * K * T + 4 * P * SLOTS + E * (2 * K * H + H * N) * 17 // 32 + 2 * P * (SLOTS + 2 * T) // PER_COLUMN + 4 * N * T
 
-VECTOR_SLOTS = 3 * P
-SCALAR_PIECES = ((VECTOR_SLOTS, 4 * P + 32), (4 * P + 32, SLOTS))
+VECTOR_SLOTS = 3 * P - 32
+SCALAR_PIECES = ((VECTOR_SLOTS, 6 * P), (6 * P, SLOTS))
 
 F32 = mybir.dt.float32
 BF16 = mybir.dt.bfloat16
@@ -58,7 +58,6 @@ def tile_moe_pre_glu_silu_kernel(
         s2_sb = keep.tile([P, E * H_PASSES, N], U8, name="s2_sb", align_bytes=64)
         weighted = keep.tile([P, PACK, VECTOR_SLOTS], F32, name="weighted")
         plain = [keep.tile([P, PACK, hi - lo], F32, name="plain%d" % lo) for lo, hi in SCALAR_PIECES]
-        x_bf16 = keep.tile([P, SLOTS * PACK], BF16, name="x_bf16", align_bytes=64)
         identity = keep.tile([P, P], F32, name="identity")
         y_sb = keep.tile([P, SLOTS], F32, name="y_sb")
         warm = keep.tile([P, 2], F32, name="warm")
@@ -67,10 +66,9 @@ def tile_moe_pre_glu_silu_kernel(
             by_pass = words.rearrange("e s p n -> p (e s) n")
             nc.sync.dma_start(out=tile.bitcast(I32), in_=by_pass[:, lo:hi, :].bitcast(I32))
 
-        def load_scales(tile, scales):
+        def load_scale_row(r, tile, scales, lo, hi):
             rows = scales.rearrange("e s (q r) n -> r q (e s) n", r=SCALE_ROWS)
-            for r in range(SCALE_ROWS):
-                nc.sync.dma_start(out=tile[r:P:QUADRANT, :, :].bitcast(I32), in_=rows[r].bitcast(I32))
+            nc.sync.dma_start(out=tile[r:P:QUADRANT, :, :].bitcast(I32), in_=rows[r][:, lo:hi, :].bitcast(I32))
 
         def load_gate(lo, hi):
             nc.sync.dma_start(out=gate_sb[:, lo:hi], in_=gate[0:P, lo:hi])
@@ -87,16 +85,23 @@ def tile_moe_pre_glu_silu_kernel(
         for d in range(1, PACK):
             nc.sync.dma_start(out=x_rows[d][:], in_=x_by_d[d])
         load_words(w1_sb[:, 0:1, :], w1_words, 0, 1)
-        load_scales(s1_sb, w1_scales)
-        load_gate(VECTOR_SLOTS, SLOTS)
+        load_gate(VECTOR_SLOTS, 4 * P)
+        for r in range(2):
+            load_scale_row(r, s3_sb, w3_scales, 0, E)
+        for r in range(SCALE_ROWS):
+            load_scale_row(r, s1_sb, w1_scales, 0, E)
         load_words(w3_sb[:, 0:1, :], w3_words, 0, 1)
-        load_scales(s3_sb, w3_scales)
+        load_gate(4 * P, 6 * P)
+        for r in range(2, SCALE_ROWS):
+            load_scale_row(r, s3_sb, w3_scales, 0, E)
         load_words(w1_sb[:, 1:2, :], w1_words, 1, 2)
         load_words(w3_sb[:, 1:2, :], w3_words, 1, 2)
+        load_gate(6 * P, SLOTS)
         load_words(w1_sb[:, 2:E, :], w1_words, 2, E)
         load_words(w3_sb[:, 2:E, :], w3_words, 2, E)
         load_words(w2_sb[:], w2_words, 0, E * H_PASSES)
-        load_scales(s2_sb, w2_scales)
+        for r in range(SCALE_ROWS):
+            load_scale_row(r, s2_sb, w2_scales, 0, E * H_PASSES)
         nc.sync.dma_start(pos1_sb[:], pos1)
         nc.sync.dma_start(pos2_sb[:], pos2)
         make_identity(nc, identity[:])
@@ -118,8 +123,17 @@ def tile_moe_pre_glu_silu_kernel(
         def gather_plain(piece, d):
             nc.scalar.activation(plain[piece][:, d, :], tokens(d, *SCALAR_PIECES[piece]), COPY)
 
+        x_bf16 = {}
+
+        def open_x(first, count, tag):
+            x_bf16[first] = work.tile([P, count * PACK], BF16, name="x_bf16", tag=tag, align_bytes=64)
+
+        def x_columns(lo, hi):
+            first = max(f for f in x_bf16 if f <= lo)
+            return x_bf16[first][:, (lo - first) * PACK:(hi - first) * PACK]
+
         def interleaved(lo, hi):
-            return x_bf16[:, lo * PACK:hi * PACK].rearrange("p (c two d) -> p c d two", two=2, d=PACK)
+            return x_columns(lo, hi).rearrange("p (c two d) -> p c d two", two=2, d=PACK)
 
         def by_pairs(rows):
             return rows.rearrange("p d (c two) -> p c d two", two=2)
@@ -127,17 +141,17 @@ def tile_moe_pre_glu_silu_kernel(
         def round_x(lo, hi):
             nc.vector.tensor_copy(out=interleaved(lo, hi), in_=by_pairs(weighted[:, :, lo:hi]))
 
-        def weigh_and_round(piece, lo, hi):
+        def weigh_and_round(piece, lo, hi, engine=nc.vector):
             base = SCALAR_PIECES[piece][0]
             weights = gate_sb[:, lo:hi].rearrange("p (c two) -> p c two", two=2).unsqueeze(2)
-            nc.vector.tensor_tensor(
+            engine.tensor_tensor(
                 interleaved(lo, hi), by_pairs(plain[piece][:, :, lo - base:hi - base]),
                 weights.to_broadcast([P, (hi - lo) // 2, PACK, 2]), MULT,
             )
 
-        def quantise_x(first, count):
-            values = x_bf16[:, first * PASS:(first + count) * PASS]
-            for c, operand in enumerate(quantise(values, count * P, "x%d" % first)):
+        def quantise_x(first, count, tag=None):
+            values = x_columns(first * P, (first + count) * P)
+            for c, operand in enumerate(quantise(values, count * P, "x%d" % first, tag)):
                 x_mx[first + c] = operand
 
         def first_product(unit, words, scales, bank):
@@ -157,8 +171,13 @@ def tile_moe_pre_glu_silu_kernel(
             act_of[unit] = act[:].rearrange("j (u p v) -> j u p v", u=2, v=2)
             nc.scalar.activation(out=act_of[unit], in_=sums, func=SILU)
 
+        free_banks = ["b%d" % c for c in range(5)]
+        bank_of = {}
+
         def linear(unit):
-            b_of[unit] = first_product(unit, w3_sb, s3_sb, "b%d" % (unit % 3))
+            bank_of[unit] = free_banks[0]
+            free_banks.remove(bank_of[unit])
+            b_of[unit] = first_product(unit, w3_sb, s3_sb, bank_of[unit])
 
         def multiply(unit):
             h = work.tile([P, PASS], BF16, name="h", tag="h%d" % unit)
@@ -199,59 +218,78 @@ def tile_moe_pre_glu_silu_kernel(
                         lhsT=w2_sb[:, e * H_PASSES + s, :].bitcast(FP4X4), lhsT_scale=s2_sb[:, e * H_PASSES + s, :],
                         rhs=codes, rhs_scale=scales, start=(s == 0), stop=(s == H_PASSES - 1),
                     )
-            copy(out=y_sb[:, first * P:(first + count) * P], in_=bank[:])
+            return lambda: copy(out=y_sb[:, first * P:(first + count) * P], in_=bank[:])
 
-        for d in range(PACK):
+        nc.vector.tensor_copy(plain[1][:, 0, :], tokens(0, *SCALAR_PIECES[1]))
+        gather_plain(0, 0)
+        for d in range(1, PACK):
             for piece in range(2):
                 gather_plain(piece, d)
         for d in range(PACK - 1):
             gather_weighted(d, 0, VECTOR_SLOTS)
         for lo, hi in ((0, P), (P, VECTOR_SLOTS)):
             gather_weighted(PACK - 1, lo, hi)
+        open_x(0, 6 * P, "x_first")
         for lo, hi in ((0, P), (P, VECTOR_SLOTS)):
             round_x(lo, hi)
         quantise_x(0, 1)
-        quantise_x(1, 2)
-        weigh_and_round(0, *SCALAR_PIECES[0])
-        quantise_x(3, 1)
-        weigh_and_round(1, *SCALAR_PIECES[1])
-        lead = 8
-        for unit in range(lead):
+        weigh_and_round(0, VECTOR_SLOTS, 4 * P)
+        quantise_x(1, 1)
+        quantise_x(2, 2)
+        weigh_and_round(0, 4 * P, 6 * P)
+        for unit in range(8):
             activate(unit)
-            if 3 <= unit < 6:
+            if unit >= 3:
                 linear(unit - 3)
 
+        pending = list(range(5, UNITS))
         for unit in range(UNITS):
             multiply(unit)
-            if unit == 0:
-                quantise_x(4, 4)
-            if unit in (7, 11):
-                quantise_h(unit - 7)
-            if unit + 3 < UNITS:
-                linear(unit + 3)
+            if unit == 1:
+                quantise_x(4, 2, tag="act0")
+            if unit == 4:
+                open_x(6 * P, 2 * P, "act3")
+                weigh_and_round(1, 6 * P, SLOTS)
+            if unit == 5:
+                quantise_x(6, 2)
+            if unit == 8:
+                quantise_h(0, tag="act7")
+            if unit == 13:
+                quantise_h(4, tag="act12")
             if unit >= UNITS - 2:
-                turn(unit, 1, "t%d" % (unit % 2))
-            elif unit % 2 == 1:
-                turn(unit - 1, 2, "t%d" % (unit // 2 % 2))
-                for ahead in range(unit + lead - 1, min(unit + lead + 1, UNITS)):
+                turn(unit, 1, bank_of[unit])
+            elif unit == UNITS - 3:
+                turn(unit - 1, 2, bank_of[unit])
+            elif unit % 4 == 3:
+                turn(unit - 3, 2, bank_of[unit])
+                turn(unit - 1, 2, bank_of[unit - 1])
+                if unit + 5 < UNITS:
+                    free_banks.extend([bank_of[unit], bank_of[unit - 1]])
+                for ahead in range(unit + 5, min(unit + 9, UNITS)):
                     activate(ahead)
+            elif unit % 4 < 2:
+                free_banks.append(bank_of[unit])
+            for ahead in pending[:len(free_banks)]:
+                pending.remove(ahead)
+                linear(ahead)
+        empty_first = second_product(0, 4, "a1", nc.vector.tensor_copy)
         quantise_h(8, tag="act14")
-        second_product(0, 4, "a1")
         quantise_h(12)
-        second_product(4, 3, "a2")
+        second_product(4, 3, "a2")()
         quantise_h(14)
         quantise_h(15)
-        second_product(7, 1, "a0")
+        second_product(7, 1, "a0")()
+        empty_first()
 
-        pieces = ((0, P), (P, 2 * P), (2 * P, T))
-        columns = [slice(lo // PER_COLUMN, hi // PER_COLUMN) for lo, hi in pieces]
-        y1 = [work.tile([P, hi - lo], F32, name="y1_%d" % lo) for lo, hi in pieces]
-        total = [work.tile([P, 2 * P], F32, name="total%d" % half) for half in range(2)]
-        nc.vector.tensor_copy(y1[1][:], y_sb[:].indirect(pos1_sb[:, columns[1]]))
-        for c in (0, 2):
+        half = T // 2
+        columns = [slice(c * half // PER_COLUMN, (c + 1) * half // PER_COLUMN) for c in range(2)]
+        y1 = [work.tile([P, half], F32, name="y1_%d" % c) for c in range(2)]
+        y2 = work.tile([P, half], F32, name="y2")
+        total = [work.tile([P, half], F32, name="total%d" % c) for c in range(2)]
+        for c in range(2):
             nc.scalar.activation(y1[c][:], y_sb[:].indirect(pos1_sb[:, columns[c]]), COPY)
-        for c, (lo, hi) in enumerate(pieces):
-            half, first = divmod(lo, 2 * P)
-            nc.vector.tensor_tensor(total[half][:, first:first + hi - lo], y_sb[:].indirect(pos2_sb[:, columns[c]]), y1[c][:], ADD)
-            if c > 0:
-                nc.sync.dma_start(out=out[:, 2 * P * half:2 * P * (half + 1)], in_=total[half][:])
+        nc.vector.tensor_copy(y2[:], y_sb[:].indirect(pos2_sb[:, columns[1]]))
+        nc.vector.tensor_tensor(total[0][:], y_sb[:].indirect(pos2_sb[:, columns[0]]), y1[0][:], ADD)
+        nc.vector.tensor_tensor(total[1][:], y2[:], y1[1][:], ADD)
+        for c in range(2):
+            nc.sync.dma_start(out=out[:, c * half:(c + 1) * half], in_=total[c][:])

@@ -10,17 +10,17 @@ PACK = 4
 PASS = P * PACK
 H_PASSES = H // PASS
 TILES_PER_EXPERT = C // P
+UNITS_PER_EXPERT = TILES_PER_EXPERT * H_PASSES
 TILES = SLOTS // P
 UNITS = TILES * H_PASSES
 PER_COLUMN = 16
 QUADRANT = 32
 SCALE_ROWS = 4
 
+STEP = 2 * PASS
+
 FLOPS = 2 * SLOTS * (2 * K * H + H * N)
 BYTES = 4 * K * T + 4 * P * SLOTS + E * (2 * K * H + H * N) * 17 // 32 + 2 * P * (SLOTS + 2 * T) // PER_COLUMN + 4 * N * T
-
-VECTOR_SLOTS = 3 * P - 32
-SCALAR_PIECES = ((VECTOR_SLOTS, 6 * P), (6 * P, SLOTS))
 
 F32 = mybir.dt.float32
 BF16 = mybir.dt.bfloat16
@@ -43,21 +43,22 @@ def tile_moe_pre_glu_silu_kernel(
     with ExitStack() as ctx:
         keep = ctx.enter_context(tc.tile_pool(name="keep", bufs=1))
         work = ctx.enter_context(tc.tile_pool(name="work", bufs=1))
+        chain = ctx.enter_context(tc.tile_pool(name="chain", bufs=1))
         psum = ctx.enter_context(tc.psum_pool(name="psum", bufs=1))
 
         offs_sb = keep.tile([P, SLOTS // PER_COLUMN], U16, name="offs_sb")
         pos1_sb = keep.tile([P, T // PER_COLUMN], U16, name="pos1_sb")
         pos2_sb = keep.tile([P, T // PER_COLUMN], U16, name="pos2_sb")
         x_rows = [keep.tile([P, T], F32, name="x_rows%d" % d) for d in range(PACK)]
-        gate_sb = keep.tile([P, SLOTS], F32, name="gate_sb")
-        w1_sb = keep.tile([P, E, 2 * H], U8, name="w1_sb", align_bytes=64)
-        w3_sb = keep.tile([P, E, 2 * H], U8, name="w3_sb", align_bytes=64)
+        weighted = keep.tile([P, PACK, C], F32, name="weighted")
+        staged = {e: keep.tile([P, PACK, C], F32, name="staged%d" % e)[:] for e in (2, 3)}
+        gate_of = [keep.tile([P, C], F32, name="gate%d" % e)[:] for e in range(E)]
+        w1_sb = [keep.tile([P, 2 * H], U8, name="w1_sb%d" % e, align_bytes=64) for e in range(E)]
+        w3_sb = [keep.tile([P, 2 * H], U8, name="w3_sb%d" % e, align_bytes=64) for e in range(E)]
         w2_sb = keep.tile([P, E * H_PASSES, 2 * N], U8, name="w2_sb", align_bytes=64)
         s1_sb = keep.tile([P, E, H], U8, name="s1_sb", align_bytes=64)
         s3_sb = keep.tile([P, E, H], U8, name="s3_sb", align_bytes=64)
         s2_sb = keep.tile([P, E * H_PASSES, N], U8, name="s2_sb", align_bytes=64)
-        weighted = keep.tile([P, PACK, VECTOR_SLOTS], F32, name="weighted")
-        plain = [keep.tile([P, PACK, hi - lo], F32, name="plain%d" % lo) for lo, hi in SCALAR_PIECES]
         identity = keep.tile([P, P], F32, name="identity")
         y_sb = keep.tile([P, SLOTS], F32, name="y_sb")
         warm = keep.tile([P, 2], F32, name="warm")
@@ -66,12 +67,16 @@ def tile_moe_pre_glu_silu_kernel(
             by_pass = words.rearrange("e s p n -> p (e s) n")
             nc.sync.dma_start(out=tile.bitcast(I32), in_=by_pass[:, lo:hi, :].bitcast(I32))
 
-        def load_scale_row(r, tile, scales, lo, hi):
-            rows = scales.rearrange("e s (q r) n -> r q (e s) n", r=SCALE_ROWS)
-            nc.sync.dma_start(out=tile[r:P:QUADRANT, :, :].bitcast(I32), in_=rows[r][:, lo:hi, :].bitcast(I32))
+        def load_first_words(tiles, words, e):
+            nc.sync.dma_start(out=tiles[e][:].bitcast(I32), in_=words.rearrange("e s p n -> (e s) p n")[e].bitcast(I32))
 
-        def load_gate(lo, hi):
-            nc.sync.dma_start(out=gate_sb[:, lo:hi], in_=gate[0:P, lo:hi])
+        def load_scales(tile, scales):
+            rows = scales.rearrange("e s (q r) n -> r q (e s) n", r=SCALE_ROWS)
+            for r in range(SCALE_ROWS):
+                nc.sync.dma_start(out=tile[r:P:QUADRANT, :, :].bitcast(I32), in_=rows[r].bitcast(I32))
+
+        def load_gate(e):
+            nc.sync.dma_start(out=gate_of[e], in_=gate[0:P, e * C:(e + 1) * C])
 
         for tile in (s1_sb, s3_sb, s2_sb):
             nc.vector.memset(tile[:].rearrange("p a n -> p (a n)").bitcast(I32), 0)
@@ -81,78 +86,64 @@ def tile_moe_pre_glu_silu_kernel(
         x_by_d = xT.rearrange("(p d) t -> d p t", d=PACK)
         nc.sync.dma_start(out=x_rows[0][:], in_=x_by_d[0])
         nc.sync.dma_start(offs_sb[:], offs)
-        load_gate(0, VECTOR_SLOTS)
+        load_gate(0)
         for d in range(1, PACK):
             nc.sync.dma_start(out=x_rows[d][:], in_=x_by_d[d])
-        load_words(w1_sb[:, 0:1, :], w1_words, 0, 1)
-        load_gate(VECTOR_SLOTS, 4 * P)
-        for r in range(2):
-            load_scale_row(r, s3_sb, w3_scales, 0, E)
-        for r in range(SCALE_ROWS):
-            load_scale_row(r, s1_sb, w1_scales, 0, E)
-        load_words(w3_sb[:, 0:1, :], w3_words, 0, 1)
-        load_gate(4 * P, 6 * P)
-        for r in range(2, SCALE_ROWS):
-            load_scale_row(r, s3_sb, w3_scales, 0, E)
-        load_words(w1_sb[:, 1:2, :], w1_words, 1, 2)
-        load_words(w3_sb[:, 1:2, :], w3_words, 1, 2)
-        load_gate(6 * P, SLOTS)
-        load_words(w1_sb[:, 2:E, :], w1_words, 2, E)
-        load_words(w3_sb[:, 2:E, :], w3_words, 2, E)
+        load_first_words(w1_sb, w1_words, 0)
+        load_gate(1)
+        load_scales(s1_sb, w1_scales)
+        load_first_words(w3_sb, w3_words, 0)
+        load_scales(s3_sb, w3_scales)
+        for e in range(1, E):
+            if e + 1 < E:
+                load_gate(e + 1)
+            load_first_words(w1_sb, w1_words, e)
+            load_first_words(w3_sb, w3_words, e)
         load_words(w2_sb[:], w2_words, 0, E * H_PASSES)
-        for r in range(SCALE_ROWS):
-            load_scale_row(r, s2_sb, w2_scales, 0, E * H_PASSES)
+        load_scales(s2_sb, w2_scales)
         nc.sync.dma_start(pos1_sb[:], pos1)
         nc.sync.dma_start(pos2_sb[:], pos2)
         make_identity(nc, identity[:])
 
-        x_mx, act_of, b_of, h_of, turned_of, h_mx = {}, {}, {}, {}, {}, {}
+        x_mx, act_of, b_of, h_of, turned_of, h_mx, bank_of = {}, {}, {}, {}, {}, {}, {}
 
-        def quantise(values, width, name, tag=None):
-            codes = work.tile([P, width], U32, name=name + "_codes", tag=tag or name + "_codes", align_bytes=64)
+        def quantise(values, width, name, tag=None, codes=None):
+            if codes is None:
+                codes = work.tile([P, width], U32, name=name + "_codes", tag=tag or name + "_codes", align_bytes=64)
             scales = work.tile([P, width], U8, name=name + "_scales", align_bytes=64)
             nc.vector.quantize_mx(out=codes[:].bitcast(FP8X4), scales=scales[:], in_=values)
-            return [(codes[:, c:c + P].bitcast(FP8X4), scales[:, c:c + P]) for c in range(0, width, P)]
+            return codes, scales
 
         def tokens(d, lo, hi):
             return x_rows[d][:].indirect(offs_sb[:, lo // PER_COLUMN:hi // PER_COLUMN])
 
-        def gather_weighted(d, lo, hi):
-            nc.vector.tensor_tensor(weighted[:, d, lo:hi], tokens(d, lo, hi), gate_sb[:, lo:hi], MULT)
+        def gather_weighted(e, d, lo, hi):
+            nc.vector.tensor_tensor(weighted[:, d, lo:hi], tokens(d, e * C + lo, e * C + hi), gate_of[e][:, lo:hi], MULT)
 
-        def gather_plain(piece, d):
-            nc.scalar.activation(plain[piece][:, d, :], tokens(d, *SCALAR_PIECES[piece]), COPY)
+        def gather_scalar(e, d):
+            nc.scalar.activation(staged[e][:, d, :], tokens(d, e * C, (e + 1) * C), COPY)
 
-        x_bf16 = {}
+        def open_x(e):
+            return chain.tile([P, C * PACK], BF16, name="x_bf16_%d" % e, align_bytes=64, offset=e * STEP)
 
-        def open_x(first, count, tag):
-            x_bf16[first] = work.tile([P, count * PACK], BF16, name="x_bf16", tag=tag, align_bytes=64)
-
-        def x_columns(lo, hi):
-            first = max(f for f in x_bf16 if f <= lo)
-            return x_bf16[first][:, (lo - first) * PACK:(hi - first) * PACK]
-
-        def interleaved(lo, hi):
-            return x_columns(lo, hi).rearrange("p (c two d) -> p c d two", two=2, d=PACK)
-
-        def by_pairs(rows):
-            return rows.rearrange("p d (c two) -> p c d two", two=2)
-
-        def round_x(lo, hi):
-            nc.vector.tensor_copy(out=interleaved(lo, hi), in_=by_pairs(weighted[:, :, lo:hi]))
-
-        def weigh_and_round(piece, lo, hi, engine=nc.vector):
-            base = SCALAR_PIECES[piece][0]
-            weights = gate_sb[:, lo:hi].rearrange("p (c two) -> p c two", two=2).unsqueeze(2)
-            engine.tensor_tensor(
-                interleaved(lo, hi), by_pairs(plain[piece][:, :, lo - base:hi - base]),
-                weights.to_broadcast([P, (hi - lo) // 2, PACK, 2]), MULT,
+        def round_x(x_bf16, lo, hi):
+            nc.vector.tensor_copy(
+                out=x_bf16[:, lo * PACK:hi * PACK].rearrange("p (c two d) -> p c d two", two=2, d=PACK),
+                in_=weighted[:, :, lo:hi].rearrange("p d (c two) -> p c d two", two=2),
             )
 
-        def quantise_x(first, count, tag=None):
-            values = x_columns(first * P, (first + count) * P)
-            for c, operand in enumerate(quantise(values, count * P, "x%d" % first, tag)):
-                x_mx[first + c] = operand
+        def weigh_and_round(e):
+            x_bf16 = open_x(e)
+            nc.gpsimd.tensor_tensor(
+                x_bf16[:].rearrange("p (c d) -> p c d", d=PACK), staged[e].rearrange("p d c -> p c d"),
+                gate_of[e].unsqueeze(2).to_broadcast([P, C, PACK]), MULT,
+            )
+            return x_bf16
+
+        def quantise_x(values, first, count, tag=None):
+            codes, scales = quantise(values, count * P, "x%d" % first, tag)
+            for c in range(count):
+                x_mx[first + c] = (codes[:, c * P:(c + 1) * P].bitcast(FP8X4), scales[:, c * P:(c + 1) * P])
 
         def first_product(unit, words, scales, bank):
             j, s = divmod(unit, H_PASSES)
@@ -160,126 +151,147 @@ def tile_moe_pre_glu_silu_kernel(
             sums = psum.tile([P, PASS], F32, name="sums", tag=bank)
             nc.tensor.matmul_mx(
                 out=sums[:], lhsT=x_mx[j][0], lhsT_scale=x_mx[j][1],
-                rhs=words[:, e, 2 * PASS * s:2 * PASS * (s + 1)].bitcast(FP4X4),
+                rhs=words[e][:, 2 * PASS * s:2 * PASS * (s + 1)].bitcast(FP4X4),
                 rhs_scale=scales[:, e, PASS * s:PASS * (s + 1)], start=True, stop=True,
             )
             return sums[:].rearrange("j (p u v) -> j u p v", u=2, v=2)
 
-        def activate(unit):
-            sums = first_product(unit, w1_sb, s1_sb, "a%d" % (unit % 3))
+        def activate(unit, bank=None):
+            sums = first_product(unit, w1_sb, s1_sb, bank or "a%d" % (unit % 3))
             act = work.tile([P, PASS], F32, name="act", tag="act%d" % unit, align_bytes=64)
             act_of[unit] = act[:].rearrange("j (u p v) -> j u p v", u=2, v=2)
             nc.scalar.activation(out=act_of[unit], in_=sums, func=SILU)
 
-        free_banks = ["b%d" % c for c in range(5)]
-        bank_of = {}
+        def linear(unit, bank):
+            bank_of[unit] = bank
+            b_of[unit] = first_product(unit, w3_sb, s3_sb, bank)
 
-        def linear(unit):
-            bank_of[unit] = free_banks[0]
-            free_banks.remove(bank_of[unit])
-            b_of[unit] = first_product(unit, w3_sb, s3_sb, bank_of[unit])
-
-        def multiply(unit):
-            h = work.tile([P, PASS], BF16, name="h", tag="h%d" % unit)
+        def multiply(unit, behind=None):
+            if behind is None:
+                h = work.tile([P, PASS], BF16, name="h", tag="h%d" % unit)
+            else:
+                h = chain.tile([P, PASS], BF16, name="h%d" % unit, align_bytes=64, offset=behind * STEP)
             nc.vector.tensor_tensor(h[:].rearrange("j (u p v) -> j u p v", u=2, v=2), act_of[unit], b_of[unit], MULT)
             h_of[unit] = h[:].bitcast(F32)
 
-        groups = [(0, 4), (4, 4), (8, 4), (12, 2), (14, 1), (15, 1)]
-        group_of = {u: g for g in groups for u in range(g[0], g[0] + g[1])}
-
-        def turn(unit, count, bank_tag):
-            bank = psum.tile([P, count, 2, P], F32, name="turn_bank", tag=bank_tag)
-            for s in range(count):
+        def turn(units, bank_tag, target):
+            bank = psum.tile([P, len(units), 2, P], F32, name="turn_bank", tag=bank_tag)
+            for s, unit in enumerate(units):
                 for u in range(2):
-                    nc.tensor.transpose(bank[:, s, u, :], h_of[unit + s][:, u * P:(u + 1) * P], identity[:])
-            first, units = group_of[unit]
-            if unit == first:
-                turned_of[first] = work.tile([P, units * PASS], BF16, name="h_turned", tag="h_turned%d" % first, align_bytes=64)
-            lo = (unit - first) * PASS
-            nc.scalar.copy(
-                out=turned_of[first][:, lo:lo + count * PASS].bitcast(F32).rearrange("p (s c u) -> p s c u", s=count, u=2),
-                in_=bank[:].rearrange("p s u c -> p s c u"),
-            )
+                    nc.tensor.transpose(bank[:, s, u, :], h_of[unit][:, u * P:(u + 1) * P], identity[:])
+            nc.scalar.copy(out=target, in_=bank[:].rearrange("p s u c -> p s c u"))
 
-        def quantise_h(first, tag=None):
-            units = group_of[first][1]
-            for c, operand in enumerate(quantise(turned_of[first][:], units * P, "h%d" % first, tag)):
-                h_mx[first + c] = operand
+        def open_turned(name, passes, slots):
+            tile = work.tile([P, passes * slots * PACK], BF16, name=name, align_bytes=64)
+            turned_of[name] = tile
+            return tile[:].bitcast(F32).rearrange("p (s c u) -> p s c u", s=passes, u=2)
 
-        def second_product(first, count, bank_tag, copy=nc.scalar.copy):
-            bank = psum.tile([P, count * P], F32, name="y", tag=bank_tag)
-            for c in range(count):
-                j = first + c
-                e = j // TILES_PER_EXPERT
-                for s in range(H_PASSES):
-                    codes, scales = h_mx[H_PASSES * j + s]
-                    nc.tensor.matmul_mx(
-                        out=bank[:, c * P:(c + 1) * P],
-                        lhsT=w2_sb[:, e * H_PASSES + s, :].bitcast(FP4X4), lhsT_scale=s2_sb[:, e * H_PASSES + s, :],
-                        rhs=codes, rhs_scale=scales, start=(s == 0), stop=(s == H_PASSES - 1),
-                    )
-            return lambda: copy(out=y_sb[:, first * P:(first + count) * P], in_=bank[:])
+        def turn_expert(e, first_bank):
+            words = open_turned("turned%d" % e, H_PASSES, C)
+            banks = (first_bank, bank_of[UNITS_PER_EXPERT * e + 3])
+            for c in range(TILES_PER_EXPERT):
+                first = UNITS_PER_EXPERT * e + H_PASSES * c
+                turn([first, first + 1], banks[c], words[:, :, c * P:(c + 1) * P, :])
 
-        nc.vector.tensor_copy(plain[1][:, 0, :], tokens(0, *SCALAR_PIECES[1]))
-        gather_plain(0, 0)
-        for d in range(1, PACK):
-            for piece in range(2):
-                gather_plain(piece, d)
+        def quantise_h(name, passes, slots, tag=None, codes=None):
+            codes, scales = quantise(turned_of[name][:], passes * slots, "h" + name, tag, codes)
+            return [(codes[:, s * slots:(s + 1) * slots].bitcast(FP8X4), scales[:, s * slots:(s + 1) * slots]) for s in range(passes)]
+
+        def second_product(columns, e, operands):
+            for s, (codes, scales) in enumerate(operands):
+                nc.tensor.matmul_mx(
+                    out=columns, lhsT=w2_sb[:, e * H_PASSES + s, :].bitcast(FP4X4), lhsT_scale=s2_sb[:, e * H_PASSES + s, :],
+                    rhs=codes, rhs_scale=scales, start=(s == 0), stop=(s == H_PASSES - 1),
+                )
+
+        for e in (2, 3):
+            for d in range(PACK):
+                gather_scalar(e, d)
         for d in range(PACK - 1):
-            gather_weighted(d, 0, VECTOR_SLOTS)
-        for lo, hi in ((0, P), (P, VECTOR_SLOTS)):
-            gather_weighted(PACK - 1, lo, hi)
-        open_x(0, 6 * P, "x_first")
-        for lo, hi in ((0, P), (P, VECTOR_SLOTS)):
-            round_x(lo, hi)
-        quantise_x(0, 1)
-        weigh_and_round(0, VECTOR_SLOTS, 4 * P)
-        quantise_x(1, 1)
-        quantise_x(2, 2)
-        weigh_and_round(0, 4 * P, 6 * P)
-        for unit in range(8):
+            gather_weighted(0, d, 0, C)
+        x_bf16 = open_x(0)
+        gather_weighted(0, PACK - 1, 0, P)
+        round_x(x_bf16, 0, P)
+        gather_weighted(0, PACK - 1, P, C)
+        quantise_x(x_bf16[:, 0:PASS], 0, 1)
+        round_x(x_bf16, P, C)
+        quantise_x(x_bf16[:, PASS:2 * PASS], 1, 1)
+        for d in range(PACK):
+            gather_weighted(1, d, 0, C)
+        x_bf16 = open_x(1)
+        round_x(x_bf16, 0, C)
+        quantise_x(x_bf16[:], 2, 2)
+        x_bf16 = weigh_and_round(2)
+        for unit in range(3):
             activate(unit)
-            if unit >= 3:
-                linear(unit - 3)
-
-        pending = list(range(5, UNITS))
-        for unit in range(UNITS):
-            multiply(unit)
-            if unit == 1:
-                quantise_x(4, 2, tag="act0")
-            if unit == 4:
-                open_x(6 * P, 2 * P, "act3")
-                weigh_and_round(1, 6 * P, SLOTS)
-            if unit == 5:
-                quantise_x(6, 2)
-            if unit == 8:
-                quantise_h(0, tag="act7")
-            if unit == 13:
-                quantise_h(4, tag="act12")
-            if unit >= UNITS - 2:
-                turn(unit, 1, bank_of[unit])
-            elif unit == UNITS - 3:
-                turn(unit - 1, 2, bank_of[unit])
-            elif unit % 4 == 3:
-                turn(unit - 3, 2, bank_of[unit])
-                turn(unit - 1, 2, bank_of[unit - 1])
-                if unit + 5 < UNITS:
-                    free_banks.extend([bank_of[unit], bank_of[unit - 1]])
-                for ahead in range(unit + 5, min(unit + 9, UNITS)):
-                    activate(ahead)
-            elif unit % 4 < 2:
-                free_banks.append(bank_of[unit])
-            for ahead in pending[:len(free_banks)]:
-                pending.remove(ahead)
-                linear(ahead)
-        empty_first = second_product(0, 4, "a1", nc.vector.tensor_copy)
-        quantise_h(8, tag="act14")
-        quantise_h(12)
-        second_product(4, 3, "a2")()
-        quantise_h(14)
-        quantise_h(15)
-        second_product(7, 1, "a0")()
-        empty_first()
+        activate(3, "b4")
+        for unit in range(4):
+            linear(unit, "b%d" % unit)
+        activate(4)
+        linear(4, "b4")
+        multiply(0, behind=1)
+        activate(5)
+        linear(5, bank_of[0])
+        multiply(1)
+        activate(6)
+        linear(6, bank_of[1])
+        multiply(2)
+        activate(7)
+        linear(7, bank_of[2])
+        multiply(3)
+        turn_expert(0, "a0")
+        multiply(4)
+        quantise_x(x_bf16[:], 4, 2, "act4")
+        x_bf16 = weigh_and_round(3)
+        activate(8)
+        linear(8, bank_of[4])
+        multiply(5, behind=2)
+        activate(9)
+        linear(9, bank_of[5])
+        multiply(6)
+        activate(10)
+        linear(10, bank_of[6])
+        activate(11)
+        linear(11, bank_of[3])
+        multiply(7)
+        turn_expert(1, "a1")
+        multiply(8)
+        multiply(9)
+        quantise_x(x_bf16[:], 6, 2, "act9")
+        activate(12)
+        linear(12, bank_of[8])
+        multiply(10, behind=3)
+        activate(13)
+        linear(13, bank_of[9])
+        activate(14)
+        linear(14, bank_of[10])
+        activate(15)
+        linear(15, bank_of[7])
+        multiply(11)
+        h0_codes = chain.tile([P, H_PASSES * C], U32, name="h0_codes", align_bytes=64, offset=E * STEP)
+        turn_expert(2, "a1")
+        h0 = quantise_h("turned0", H_PASSES, C, codes=h0_codes)
+        h1 = quantise_h("turned1", H_PASSES, C, tag="turned0")
+        multiply(12)
+        y_first = psum.tile([P, 2 * C], F32, name="y_first", tag="a2")
+        second_product(y_first[:, 0:C], 0, h0)
+        second_product(y_first[:, C:2 * C], 1, h1)
+        multiply(13)
+        turn([12, 13], bank_of[13], open_turned("turned6", H_PASSES, P))
+        multiply(14)
+        nc.scalar.copy(out=y_sb[:, 0:2 * C], in_=y_first[:])
+        turn([14], bank_of[14], open_turned("turned14", 1, P))
+        multiply(15)
+        turn([15], bank_of[15], open_turned("turned15", 1, P))
+        h2 = quantise_h("turned2", H_PASSES, C, tag="act15")
+        y_mid = psum.tile([P, C + P], F32, name="y_mid", tag="a1")
+        second_product(y_mid[:, 0:C], 2, h2)
+        second_product(y_mid[:, C:C + P], 3, quantise_h("turned6", H_PASSES, P))
+        nc.scalar.copy(out=y_sb[:, 2 * C:3 * C + P], in_=y_mid[:])
+        h7 = quantise_h("turned14", 1, P) + quantise_h("turned15", 1, P)
+        y_last = psum.tile([P, P], F32, name="y_last", tag="a0")
+        second_product(y_last[:], 3, h7)
+        nc.vector.tensor_copy(out=y_sb[:, 3 * C + P:SLOTS], in_=y_last[:])
 
         half = T // 2
         columns = [slice(c * half // PER_COLUMN, (c + 1) * half // PER_COLUMN) for c in range(2)]

@@ -145,6 +145,14 @@ def tile_moe_pre_glu_silu_kernel(
             for c in range(count):
                 x_mx[first + c] = (codes[:, c * P:(c + 1) * P].bitcast(FP8X4), scales[:, c * P:(c + 1) * P])
 
+        def finish_on_vector(e, x_bf16):
+            for lo in (0, P):
+                gather_weighted(e, PACK - 1, lo, lo + P)
+            for lo in (0, P):
+                round_x(x_bf16, lo, lo + P)
+            for c in range(TILES_PER_EXPERT):
+                quantise_x(x_bf16[:, c * PASS:(c + 1) * PASS], TILES_PER_EXPERT * e + c, 1)
+
         def first_product(unit, words, scales, bank):
             j, s = divmod(unit, H_PASSES)
             e = j // TILES_PER_EXPERT
@@ -210,17 +218,10 @@ def tile_moe_pre_glu_silu_kernel(
         for d in range(PACK - 1):
             gather_weighted(0, d, 0, C)
         x_bf16 = open_x(0)
-        gather_weighted(0, PACK - 1, 0, P)
-        round_x(x_bf16, 0, P)
-        gather_weighted(0, PACK - 1, P, C)
-        quantise_x(x_bf16[:, 0:PASS], 0, 1)
-        round_x(x_bf16, P, C)
-        quantise_x(x_bf16[:, PASS:2 * PASS], 1, 1)
-        for d in range(PACK):
+        finish_on_vector(0, x_bf16)
+        for d in range(PACK - 1):
             gather_weighted(1, d, 0, C)
-        x_bf16 = open_x(1)
-        round_x(x_bf16, 0, C)
-        quantise_x(x_bf16[:], 2, 2)
+        finish_on_vector(1, open_x(1))
         x_bf16 = weigh_and_round(2)
         for unit in range(3):
             activate(unit)
@@ -229,7 +230,7 @@ def tile_moe_pre_glu_silu_kernel(
             linear(unit, "b%d" % unit)
         activate(4)
         linear(4, "b4")
-        multiply(0, behind=1)
+        multiply(0)
         activate(5)
         linear(5, bank_of[0])
         multiply(1)
@@ -241,14 +242,14 @@ def tile_moe_pre_glu_silu_kernel(
         multiply(3)
         turn_expert(0, "a0")
         multiply(4)
-        quantise_x(x_bf16[:], 4, 2, "act4")
+        quantise_x(x_bf16[:], 4, 2, "act3")
         x_bf16 = weigh_and_round(3)
         activate(8)
         linear(8, bank_of[4])
-        multiply(5, behind=2)
+        multiply(5)
         activate(9)
         linear(9, bank_of[5])
-        multiply(6)
+        multiply(6, behind=2)
         activate(10)
         linear(10, bank_of[6])
         activate(11)
@@ -257,21 +258,21 @@ def tile_moe_pre_glu_silu_kernel(
         turn_expert(1, "a1")
         multiply(8)
         multiply(9)
-        quantise_x(x_bf16[:], 6, 2, "act9")
+        quantise_x(x_bf16[:], 6, 2, "act8")
         activate(12)
         linear(12, bank_of[8])
-        multiply(10, behind=3)
+        multiply(10)
         activate(13)
         linear(13, bank_of[9])
         activate(14)
         linear(14, bank_of[10])
         activate(15)
         linear(15, bank_of[7])
-        multiply(11)
+        multiply(11, behind=3)
         h0_codes = chain.tile([P, H_PASSES * C], U32, name="h0_codes", align_bytes=64, offset=E * STEP)
         turn_expert(2, "a1")
         h0 = quantise_h("turned0", H_PASSES, C, codes=h0_codes)
-        h1 = quantise_h("turned1", H_PASSES, C, tag="turned0")
+        h1 = quantise_h("turned1", H_PASSES, C, tag="act11")
         multiply(12)
         y_first = psum.tile([P, 2 * C], F32, name="y_first", tag="a2")
         second_product(y_first[:, 0:C], 0, h0)
@@ -283,7 +284,7 @@ def tile_moe_pre_glu_silu_kernel(
         turn([14], bank_of[14], open_turned("turned14", 1, P))
         multiply(15)
         turn([15], bank_of[15], open_turned("turned15", 1, P))
-        h2 = quantise_h("turned2", H_PASSES, C, tag="act15")
+        h2 = quantise_h("turned2", H_PASSES, C, tag="act14")
         y_mid = psum.tile([P, C + P], F32, name="y_mid", tag="a1")
         second_product(y_mid[:, 0:C], 2, h2)
         second_product(y_mid[:, C:C + P], 3, quantise_h("turned6", H_PASSES, P))

@@ -17,6 +17,7 @@ PER_COLUMN = 16
 QUADRANT = 32
 SCALE_ROWS = 4
 
+SHARE = 64
 STEP = 2 * PASS
 
 FLOPS = 2 * SLOTS * (2 * K * H + H * N)
@@ -51,7 +52,9 @@ def tile_moe_pre_glu_silu_kernel(
         pos2_sb = keep.tile([P, T // PER_COLUMN], U16, name="pos2_sb")
         x_rows = [keep.tile([P, T], F32, name="x_rows%d" % d) for d in range(PACK)]
         weighted = keep.tile([P, PACK, C], F32, name="weighted")
-        staged = {e: keep.tile([P, PACK, C], F32, name="staged%d" % e)[:] for e in (2, 3)}
+        plain_first = keep.tile([P, PACK, SHARE + C], F32, name="plain_first")
+        plain_last = keep.tile([P, PACK, C], F32, name="plain_last")
+        staged = {2: plain_first[:, :, SHARE:], 3: plain_last[:]}
         gate_of = [keep.tile([P, C], F32, name="gate%d" % e)[:] for e in range(E)]
         w1_sb = [keep.tile([P, 2 * H], U8, name="w1_sb%d" % e, align_bytes=64) for e in range(E)]
         w3_sb = [keep.tile([P, 2 * H], U8, name="w3_sb%d" % e, align_bytes=64) for e in range(E)]
@@ -120,8 +123,8 @@ def tile_moe_pre_glu_silu_kernel(
         def gather_weighted(e, d, lo, hi):
             nc.vector.tensor_tensor(weighted[:, d, lo:hi], tokens(d, e * C + lo, e * C + hi), gate_of[e][:, lo:hi], MULT)
 
-        def gather_scalar(e, d):
-            nc.scalar.activation(staged[e][:, d, :], tokens(d, e * C, (e + 1) * C), COPY)
+        def gather_scalar(rows, d, lo, hi):
+            nc.scalar.activation(rows[:, d, :], tokens(d, lo, hi), COPY)
 
         def open_x(e):
             return chain.tile([P, C * PACK], BF16, name="x_bf16_%d" % e, align_bytes=64, offset=e * STEP)
@@ -145,11 +148,21 @@ def tile_moe_pre_glu_silu_kernel(
             for c in range(count):
                 x_mx[first + c] = (codes[:, c * P:(c + 1) * P].bitcast(FP8X4), scales[:, c * P:(c + 1) * P])
 
-        def finish_on_vector(e, x_bf16):
-            for lo in (0, P):
-                gather_weighted(e, PACK - 1, lo, lo + P)
-            for lo in (0, P):
-                round_x(x_bf16, lo, lo + P)
+        def weigh_share(x_bf16):
+            weights = gate_of[1][:, C - SHARE:].rearrange("p (c two) -> p c two", two=2).unsqueeze(2)
+            nc.vector.tensor_tensor(
+                x_bf16[:, (C - SHARE) * PACK:].rearrange("p (c two d) -> p c d two", two=2, d=PACK),
+                plain_first[:, :, :SHARE].rearrange("p d (c two) -> p c d two", two=2),
+                weights.to_broadcast([P, SHARE // 2, PACK, 2]), MULT,
+            )
+
+        def finish_on_vector(e, x_bf16, end):
+            for lo, hi in ((0, P), (P, end)):
+                gather_weighted(e, PACK - 1, lo, hi)
+            for lo, hi in ((0, P), (P, end)):
+                round_x(x_bf16, lo, hi)
+            if end < C:
+                weigh_share(x_bf16)
             for c in range(TILES_PER_EXPERT):
                 quantise_x(x_bf16[:, c * PASS:(c + 1) * PASS], TILES_PER_EXPERT * e + c, 1)
 
@@ -212,16 +225,16 @@ def tile_moe_pre_glu_silu_kernel(
                     rhs=codes, rhs_scale=scales, start=(s == 0), stop=(s == H_PASSES - 1),
                 )
 
-        for e in (2, 3):
+        for rows, lo, hi in ((plain_first, 2 * C - SHARE, 3 * C), (plain_last, 3 * C, SLOTS)):
             for d in range(PACK):
-                gather_scalar(e, d)
+                gather_scalar(rows, d, lo, hi)
         for d in range(PACK - 1):
             gather_weighted(0, d, 0, C)
         x_bf16 = open_x(0)
-        finish_on_vector(0, x_bf16)
+        finish_on_vector(0, x_bf16, C)
         for d in range(PACK - 1):
-            gather_weighted(1, d, 0, C)
-        finish_on_vector(1, open_x(1))
+            gather_weighted(1, d, 0, C - SHARE)
+        finish_on_vector(1, open_x(1), C - SHARE)
         x_bf16 = weigh_and_round(2)
         for unit in range(3):
             activate(unit)

@@ -55,9 +55,12 @@ def tile_moe_pre_glu_silu_kernel(
         plain_first = keep.tile([P, PACK, SHARE + C], F32, name="plain_first")
         plain_last = keep.tile([P, PACK, C], F32, name="plain_last")
         staged = {2: plain_first[:, :, SHARE:], 3: plain_last[:]}
-        gate_of = [keep.tile([P, C], F32, name="gate%d" % e)[:] for e in range(E)]
-        w1_sb = [keep.tile([P, 2 * H], U8, name="w1_sb%d" % e, align_bytes=64) for e in range(E)]
-        w3_sb = [keep.tile([P, 2 * H], U8, name="w3_sb%d" % e, align_bytes=64) for e in range(E)]
+        gate_late = keep.tile([P, 2 * C], F32, name="gate_late")
+        gate_of = [keep.tile([P, C], F32, name="gate%d" % e)[:] for e in range(2)] + [gate_late[:, c * C:(c + 1) * C] for c in range(2)]
+        w1_late = keep.tile([P, 2, 2 * H], U8, name="w1_late", align_bytes=64)
+        w3_late = keep.tile([P, 2, 2 * H], U8, name="w3_late", align_bytes=64)
+        w1_sb = [keep.tile([P, 2 * H], U8, name="w1_sb%d" % e, align_bytes=64)[:] for e in range(2)] + [w1_late[:, e, :] for e in range(2)]
+        w3_sb = [keep.tile([P, 2 * H], U8, name="w3_sb%d" % e, align_bytes=64)[:] for e in range(2)] + [w3_late[:, e, :] for e in range(2)]
         w2_sb = keep.tile([P, E * H_PASSES, 2 * N], U8, name="w2_sb", align_bytes=64)
         s1_sb = keep.tile([P, E, H], U8, name="s1_sb", align_bytes=64)
         s3_sb = keep.tile([P, E, H], U8, name="s3_sb", align_bytes=64)
@@ -71,15 +74,15 @@ def tile_moe_pre_glu_silu_kernel(
             nc.sync.dma_start(out=tile.bitcast(I32), in_=by_pass[:, lo:hi, :].bitcast(I32))
 
         def load_first_words(tiles, words, e):
-            nc.sync.dma_start(out=tiles[e][:].bitcast(I32), in_=words.rearrange("e s p n -> (e s) p n")[e].bitcast(I32))
+            nc.sync.dma_start(out=tiles[e].bitcast(I32), in_=words.rearrange("e s p n -> (e s) p n")[e].bitcast(I32))
 
         def load_scales(tile, scales):
             rows = scales.rearrange("e s (q r) n -> r q (e s) n", r=SCALE_ROWS)
             for r in range(SCALE_ROWS):
                 nc.sync.dma_start(out=tile[r:P:QUADRANT, :, :].bitcast(I32), in_=rows[r].bitcast(I32))
 
-        def load_gate(e):
-            nc.sync.dma_start(out=gate_of[e], in_=gate[0:P, e * C:(e + 1) * C])
+        def load_gate(columns, lo, hi):
+            nc.sync.dma_start(out=columns, in_=gate[0:P, lo:hi])
 
         for tile in (s1_sb, s3_sb, s2_sb):
             nc.vector.memset(tile[:].rearrange("p a n -> p (a n)").bitcast(I32), 0)
@@ -89,19 +92,19 @@ def tile_moe_pre_glu_silu_kernel(
         x_by_d = xT.rearrange("(p d) t -> d p t", d=PACK)
         nc.sync.dma_start(out=x_rows[0][:], in_=x_by_d[0])
         nc.sync.dma_start(offs_sb[:], offs)
-        load_gate(0)
+        load_gate(gate_of[0], 0, C)
         for d in range(1, PACK):
             nc.sync.dma_start(out=x_rows[d][:], in_=x_by_d[d])
         load_first_words(w1_sb, w1_words, 0)
-        load_gate(1)
+        load_gate(gate_of[1], C, 2 * C)
         load_scales(s1_sb, w1_scales)
         load_first_words(w3_sb, w3_words, 0)
         load_scales(s3_sb, w3_scales)
-        for e in range(1, E):
-            if e + 1 < E:
-                load_gate(e + 1)
-            load_first_words(w1_sb, w1_words, e)
-            load_first_words(w3_sb, w3_words, e)
+        load_first_words(w1_sb, w1_words, 1)
+        load_gate(gate_late[:], 2 * C, SLOTS)
+        load_first_words(w3_sb, w3_words, 1)
+        load_words(w1_late[:], w1_words, 2, E)
+        load_words(w3_late[:], w3_words, 2, E)
         load_words(w2_sb[:], w2_words, 0, E * H_PASSES)
         load_scales(s2_sb, w2_scales)
         nc.sync.dma_start(pos1_sb[:], pos1)
@@ -225,9 +228,12 @@ def tile_moe_pre_glu_silu_kernel(
                     rhs=codes, rhs_scale=scales, start=(s == 0), stop=(s == H_PASSES - 1),
                 )
 
-        for rows, lo, hi in ((plain_first, 2 * C - SHARE, 3 * C), (plain_last, 3 * C, SLOTS)):
-            for d in range(PACK):
-                gather_scalar(rows, d, lo, hi)
+        for d in range(PACK):
+            gather_scalar(plain_first, d, 2 * C - SHARE, 3 * C)
+        nc.vector.tensor_copy(plain_last[:, 0, 0:P], tokens(0, 3 * C, 3 * C + P))
+        nc.scalar.activation(plain_last[:, 0, P:C], tokens(0, 3 * C + P, SLOTS), COPY)
+        for d in range(1, PACK):
+            gather_scalar(plain_last, d, 3 * C, SLOTS)
         for d in range(PACK - 1):
             gather_weighted(0, d, 0, C)
         x_bf16 = open_x(0)
@@ -239,55 +245,56 @@ def tile_moe_pre_glu_silu_kernel(
         for unit in range(3):
             activate(unit)
         activate(3, "b4")
-        for unit in range(4):
+        for unit in range(3):
             linear(unit, "b%d" % unit)
-        activate(4)
-        linear(4, "b4")
+        activate(4, "b3")
         multiply(0)
+        linear(3, bank_of[0])
         activate(5)
-        linear(5, bank_of[0])
         multiply(1)
         activate(6)
-        linear(6, bank_of[1])
+        linear(4, "b4")
         multiply(2)
         activate(7)
+        linear(5, bank_of[1])
+        linear(6, "b3")
         linear(7, bank_of[2])
         multiply(3)
-        turn_expert(0, "a0")
+        turn_expert(0, "a2")
         multiply(4)
         quantise_x(x_bf16[:], 4, 2, "act3")
         x_bf16 = weigh_and_round(3)
-        activate(8)
+        activate(8, "a0")
         linear(8, bank_of[4])
         multiply(5)
-        activate(9)
+        activate(9, "a1")
         linear(9, bank_of[5])
         multiply(6, behind=2)
-        activate(10)
+        activate(10, "a2")
         linear(10, bank_of[6])
-        activate(11)
+        activate(11, "a0")
         linear(11, bank_of[3])
         multiply(7)
         turn_expert(1, "a1")
         multiply(8)
         multiply(9)
         quantise_x(x_bf16[:], 6, 2, "act8")
-        activate(12)
+        activate(12, "a2")
         linear(12, bank_of[8])
         multiply(10)
-        activate(13)
+        activate(13, "a0")
         linear(13, bank_of[9])
-        activate(14)
+        activate(14, "a1")
         linear(14, bank_of[10])
-        activate(15)
+        activate(15, "a2")
         linear(15, bank_of[7])
         multiply(11, behind=3)
         h0_codes = chain.tile([P, H_PASSES * C], U32, name="h0_codes", align_bytes=64, offset=E * STEP)
-        turn_expert(2, "a1")
+        turn_expert(2, "a0")
         h0 = quantise_h("turned0", H_PASSES, C, codes=h0_codes)
         h1 = quantise_h("turned1", H_PASSES, C, tag="act11")
         multiply(12)
-        y_first = psum.tile([P, 2 * C], F32, name="y_first", tag="a2")
+        y_first = psum.tile([P, 2 * C], F32, name="y_first", tag="a1")
         second_product(y_first[:, 0:C], 0, h0)
         second_product(y_first[:, C:2 * C], 1, h1)
         multiply(13)
@@ -298,24 +305,26 @@ def tile_moe_pre_glu_silu_kernel(
         multiply(15)
         turn([15], bank_of[15], open_turned("turned15", 1, P))
         h2 = quantise_h("turned2", H_PASSES, C, tag="act14")
-        y_mid = psum.tile([P, C + P], F32, name="y_mid", tag="a1")
+        y_mid = psum.tile([P, C + P], F32, name="y_mid", tag="a0")
         second_product(y_mid[:, 0:C], 2, h2)
         second_product(y_mid[:, C:C + P], 3, quantise_h("turned6", H_PASSES, P))
         nc.scalar.copy(out=y_sb[:, 2 * C:3 * C + P], in_=y_mid[:])
         h7 = quantise_h("turned14", 1, P) + quantise_h("turned15", 1, P)
-        y_last = psum.tile([P, P], F32, name="y_last", tag="a0")
+        y_last = psum.tile([P, P], F32, name="y_last", tag="a2")
         second_product(y_last[:], 3, h7)
         nc.vector.tensor_copy(out=y_sb[:, 3 * C + P:SLOTS], in_=y_last[:])
 
-        half = T // 2
-        columns = [slice(c * half // PER_COLUMN, (c + 1) * half // PER_COLUMN) for c in range(2)]
-        y1 = [work.tile([P, half], F32, name="y1_%d" % c) for c in range(2)]
-        y2 = work.tile([P, half], F32, name="y2")
-        total = [work.tile([P, half], F32, name="total%d" % c) for c in range(2)]
-        for c in range(2):
+        cuts = (0, 160, 352, T)
+        pieces = [slice(cuts[c], cuts[c + 1]) for c in range(3)]
+        columns = [slice(s.start // PER_COLUMN, s.stop // PER_COLUMN) for s in pieces]
+        y1 = [work.tile([P, s.stop - s.start], F32, name="y1_%d" % s.start) for s in pieces]
+        total = [work.tile([P, s.stop - s.start], F32, name="total%d" % s.start) for s in pieces]
+        y2 = work.tile([P, T - cuts[2]], F32, name="y2")
+        for c in range(3):
             nc.scalar.activation(y1[c][:], y_sb[:].indirect(pos1_sb[:, columns[c]]), COPY)
-        nc.vector.tensor_copy(y2[:], y_sb[:].indirect(pos2_sb[:, columns[1]]))
-        nc.vector.tensor_tensor(total[0][:], y_sb[:].indirect(pos2_sb[:, columns[0]]), y1[0][:], ADD)
-        nc.vector.tensor_tensor(total[1][:], y2[:], y1[1][:], ADD)
+        nc.vector.tensor_copy(y2[:], y_sb[:].indirect(pos2_sb[:, columns[2]]))
         for c in range(2):
-            nc.sync.dma_start(out=out[:, c * half:(c + 1) * half], in_=total[c][:])
+            nc.vector.tensor_tensor(total[c][:], y_sb[:].indirect(pos2_sb[:, columns[c]]), y1[c][:], ADD)
+        nc.vector.tensor_tensor(total[2][:], y2[:], y1[2][:], ADD)
+        for c in range(3):
+            nc.sync.dma_start(out=out[:, pieces[c]], in_=total[c][:])

@@ -17,7 +17,7 @@ PER_COLUMN = 16
 QUADRANT = 32
 SCALE_ROWS = 4
 
-SHARE = 64
+SHARE = 128
 STEP = 2 * PASS
 
 FLOPS = 2 * SLOTS * (2 * K * H + H * N)
@@ -56,7 +56,7 @@ def tile_moe_pre_glu_silu_kernel(
         plain_last = keep.tile([P, PACK, C], F32, name="plain_last")
         staged = {2: plain_first[:, :, SHARE:], 3: plain_last[:]}
         gate_late = keep.tile([P, 2 * C], F32, name="gate_late")
-        gate_of = [keep.tile([P, C], F32, name="gate%d" % e)[:] for e in range(2)] + [gate_late[:, c * C:(c + 1) * C] for c in range(2)]
+        gate_of = [plain_last[:, 1, :], keep.tile([P, C], F32, name="gate1")[:]] + [gate_late[:, c * C:(c + 1) * C] for c in range(2)]
         w1_late = keep.tile([P, 2, 2 * H], U8, name="w1_late", align_bytes=64)
         w3_late = keep.tile([P, 2, 2 * H], U8, name="w3_late", align_bytes=64)
         w1_sb = [keep.tile([P, 2 * H], U8, name="w1_sb%d" % e, align_bytes=64)[:] for e in range(2)] + [w1_late[:, e, :] for e in range(2)]
@@ -96,8 +96,9 @@ def tile_moe_pre_glu_silu_kernel(
         for d in range(1, PACK):
             nc.sync.dma_start(out=x_rows[d][:], in_=x_by_d[d])
         load_first_words(w1_sb, w1_words, 0)
-        load_gate(gate_of[1], C, 2 * C)
+        nc.sync.dma_start(pos1_sb[:], pos1)
         load_scales(s1_sb, w1_scales)
+        load_gate(gate_of[1], C, 2 * C)
         load_first_words(w3_sb, w3_words, 0)
         load_scales(s3_sb, w3_scales)
         load_first_words(w1_sb, w1_words, 1)
@@ -107,7 +108,6 @@ def tile_moe_pre_glu_silu_kernel(
         load_words(w3_late[:], w3_words, 2, E)
         load_words(w2_sb[:], w2_words, 0, E * H_PASSES)
         load_scales(s2_sb, w2_scales)
-        nc.sync.dma_start(pos1_sb[:], pos1)
         nc.sync.dma_start(pos2_sb[:], pos2)
         make_identity(nc, identity[:])
 
@@ -160,13 +160,13 @@ def tile_moe_pre_glu_silu_kernel(
             )
 
         def finish_on_vector(e, x_bf16, end):
-            for lo, hi in ((0, P), (P, end)):
-                gather_weighted(e, PACK - 1, lo, hi)
-            for lo, hi in ((0, P), (P, end)):
-                round_x(x_bf16, lo, hi)
+            for lo in range(0, end, P):
+                gather_weighted(e, PACK - 1, lo, lo + P)
             if end < C:
                 weigh_share(x_bf16)
-            for c in range(TILES_PER_EXPERT):
+            for lo in range(0, end, P):
+                round_x(x_bf16, lo, lo + P)
+            for c in (range(TILES_PER_EXPERT) if end == C else reversed(range(TILES_PER_EXPERT))):
                 quantise_x(x_bf16[:, c * PASS:(c + 1) * PASS], TILES_PER_EXPERT * e + c, 1)
 
         def first_product(unit, words, scales, bank):
@@ -232,12 +232,13 @@ def tile_moe_pre_glu_silu_kernel(
             gather_scalar(plain_first, d, 2 * C - SHARE, 3 * C)
         nc.vector.tensor_copy(plain_last[:, 0, 0:P], tokens(0, 3 * C, 3 * C + P))
         nc.scalar.activation(plain_last[:, 0, P:C], tokens(0, 3 * C + P, SLOTS), COPY)
-        for d in range(1, PACK):
+        for d in range(2, PACK):
             gather_scalar(plain_last, d, 3 * C, SLOTS)
         for d in range(PACK - 1):
             gather_weighted(0, d, 0, C)
         x_bf16 = open_x(0)
         finish_on_vector(0, x_bf16, C)
+        nc.vector.tensor_copy(plain_last[:, 1, :], tokens(1, 3 * C, SLOTS))
         for d in range(PACK - 1):
             gather_weighted(1, d, 0, C - SHARE)
         finish_on_vector(1, open_x(1), C - SHARE)

@@ -57,14 +57,14 @@ def tile_moe_pre_glu_silu_kernel(
         staged = {2: plain_first[:, :, SHARE:], 3: plain_last[:]}
         gate_late = keep.tile([P, 2 * C], F32, name="gate_late")
         gate_of = [plain_last[:, 1, :], keep.tile([P, C], F32, name="gate1")[:]] + [gate_late[:, c * C:(c + 1) * C] for c in range(2)]
-        w1_late = keep.tile([P, 2, 2 * H], U8, name="w1_late", align_bytes=64)
-        w3_late = keep.tile([P, 2, 2 * H], U8, name="w3_late", align_bytes=64)
-        w1_sb = [keep.tile([P, 2 * H], U8, name="w1_sb%d" % e, align_bytes=64)[:] for e in range(2)] + [w1_late[:, e, :] for e in range(2)]
-        w3_sb = [keep.tile([P, 2 * H], U8, name="w3_sb%d" % e, align_bytes=64)[:] for e in range(2)] + [w3_late[:, e, :] for e in range(2)]
-        w2_sb = keep.tile([P, E * H_PASSES, 2 * N], U8, name="w2_sb", align_bytes=64)
-        s1_sb = keep.tile([P, E, H], U8, name="s1_sb", align_bytes=64)
-        s3_sb = keep.tile([P, E, H], U8, name="s3_sb", align_bytes=64)
-        s2_sb = keep.tile([P, E * H_PASSES, N], U8, name="s2_sb", align_bytes=64)
+        w1_late = keep.tile([P, 2, 2 * H], U8, name="w1_late", align_bytes=256)
+        w3_late = keep.tile([P, 2, 2 * H], U8, name="w3_late", align_bytes=256)
+        w1_sb = [keep.tile([P, 2 * H], U8, name="w1_sb%d" % e, align_bytes=256)[:] for e in range(2)] + [w1_late[:, e, :] for e in range(2)]
+        w3_sb = [keep.tile([P, 2 * H], U8, name="w3_sb%d" % e, align_bytes=256)[:] for e in range(2)] + [w3_late[:, e, :] for e in range(2)]
+        w2_sb = keep.tile([P, E * H_PASSES, 2 * N], U8, name="w2_sb", align_bytes=256)
+        s1_sb = keep.tile([P, E, H], U8, name="s1_sb", align_bytes=256)
+        s3_sb = keep.tile([P, E, H], U8, name="s3_sb", align_bytes=256)
+        s2_sb = keep.tile([P, E * H_PASSES, N], U8, name="s2_sb", align_bytes=256)
         identity = keep.tile([P, P], F32, name="identity")
         y_sb = keep.tile([P, SLOTS], F32, name="y_sb")
         warm = keep.tile([P, 2], F32, name="warm")
@@ -115,8 +115,8 @@ def tile_moe_pre_glu_silu_kernel(
 
         def quantise(values, width, name, tag=None, codes=None):
             if codes is None:
-                codes = work.tile([P, width], U32, name=name + "_codes", tag=tag or name + "_codes", align_bytes=64)
-            scales = work.tile([P, width], U8, name=name + "_scales", align_bytes=64)
+                codes = work.tile([P, width], U32, name=name + "_codes", tag=tag or name + "_codes", align_bytes=256)
+            scales = work.tile([P, width], U8, name=name + "_scales", align_bytes=256)
             nc.vector.quantize_mx(out=codes[:].bitcast(FP8X4), scales=scales[:], in_=values)
             return codes, scales
 
@@ -130,7 +130,7 @@ def tile_moe_pre_glu_silu_kernel(
             nc.scalar.activation(rows[:, d, :], tokens(d, lo, hi), COPY)
 
         def open_x(e):
-            return chain.tile([P, C * PACK], BF16, name="x_bf16_%d" % e, align_bytes=64, offset=e * STEP)
+            return chain.tile([P, C * PACK], BF16, name="x_bf16_%d" % e, align_bytes=256, offset=e * STEP)
 
         def round_x(x_bf16, lo, hi):
             nc.vector.tensor_copy(
@@ -182,7 +182,7 @@ def tile_moe_pre_glu_silu_kernel(
 
         def activate(unit, bank=None):
             sums = first_product(unit, w1_sb, s1_sb, bank or "a%d" % (unit % 3))
-            act = work.tile([P, PASS], F32, name="act", tag="act%d" % unit, align_bytes=64)
+            act = work.tile([P, PASS], F32, name="act", tag="act%d" % unit, align_bytes=256)
             act_of[unit] = act[:].rearrange("j (u p v) -> j u p v", u=2, v=2)
             nc.scalar.activation(out=act_of[unit], in_=sums, func=SILU)
 
@@ -194,7 +194,7 @@ def tile_moe_pre_glu_silu_kernel(
             if behind is None:
                 h = work.tile([P, PASS], BF16, name="h", tag="h%d" % unit)
             else:
-                h = chain.tile([P, PASS], BF16, name="h%d" % unit, align_bytes=64, offset=behind * STEP)
+                h = chain.tile([P, PASS], BF16, name="h%d" % unit, align_bytes=256, offset=behind * STEP)
             nc.vector.tensor_tensor(h[:].rearrange("j (u p v) -> j u p v", u=2, v=2), act_of[unit], b_of[unit], MULT)
             h_of[unit] = h[:].bitcast(F32)
 
@@ -206,7 +206,7 @@ def tile_moe_pre_glu_silu_kernel(
             nc.scalar.copy(out=target, in_=bank[:].rearrange("p s u c -> p s c u"))
 
         def open_turned(name, passes, slots):
-            tile = work.tile([P, passes * slots * PACK], BF16, name=name, align_bytes=64)
+            tile = work.tile([P, passes * slots * PACK], BF16, name=name, align_bytes=256)
             turned_of[name] = tile
             return tile[:].bitcast(F32).rearrange("p (s c u) -> p s c u", s=passes, u=2)
 
@@ -290,7 +290,7 @@ def tile_moe_pre_glu_silu_kernel(
         activate(15, "a2")
         linear(15, bank_of[7])
         multiply(11, behind=3)
-        h0_codes = chain.tile([P, H_PASSES * C], U32, name="h0_codes", align_bytes=64, offset=E * STEP)
+        h0_codes = chain.tile([P, H_PASSES * C], U32, name="h0_codes", align_bytes=256, offset=E * STEP)
         turn_expert(2, "a0")
         h0 = quantise_h("turned0", H_PASSES, C, codes=h0_codes)
         h1 = quantise_h("turned1", H_PASSES, C, tag="act11")

@@ -58,14 +58,15 @@ def tile_moe_pre_glu_silu_kernel(
         gate_late = keep.tile([P, 2 * C], F32, name="gate_late")
         gate_of = [plain_last[:, 1, :], keep.tile([P, C], F32, name="gate1")[:]] + [gate_late[:, c * C:(c + 1) * C] for c in range(2)]
         w1_late = keep.tile([P, 2, 2 * H], U8, name="w1_late", align_bytes=256)
-        w3_late = keep.tile([P, 2, 2 * H], U8, name="w3_late", align_bytes=256)
         w1_sb = [keep.tile([P, 2 * H], U8, name="w1_sb%d" % e, align_bytes=256)[:] for e in range(2)] + [w1_late[:, e, :] for e in range(2)]
-        w3_sb = [keep.tile([P, 2 * H], U8, name="w3_sb%d" % e, align_bytes=256)[:] for e in range(2)] + [w3_late[:, e, :] for e in range(2)]
+        w3_sb = [keep.tile([P, 2 * H], U8, name="w3_sb%d" % e, align_bytes=256)[:] for e in range(E)]
         w2_sb = keep.tile([P, E * H_PASSES, 2 * N], U8, name="w2_sb", align_bytes=256)
-        s1_sb = keep.tile([P, E, H], U8, name="s1_sb", align_bytes=256)
-        s3_sb = keep.tile([P, E, H], U8, name="s3_sb", align_bytes=256)
+        s1_halves = [keep.tile([P, E // 2, H], U8, name="s1_half%d" % c, align_bytes=256) for c in range(2)]
+        s1_sb = [s1_halves[e // 2][:, e % 2, :] for e in range(E)]
+        s3_all = keep.tile([P, E, H], U8, name="s3_all", align_bytes=256)
+        s3_sb = [s3_all[:, e, :] for e in range(E)]
         s2_sb = keep.tile([P, E * H_PASSES, N], U8, name="s2_sb", align_bytes=256)
-        identity = keep.tile([P, P], F32, name="identity")
+        identity = keep.tile([P, P], F32, name="identity", align_bytes=256)
         y_sb = keep.tile([P, SLOTS], F32, name="y_sb")
         warm = keep.tile([P, 2], F32, name="warm")
 
@@ -76,15 +77,15 @@ def tile_moe_pre_glu_silu_kernel(
         def load_first_words(tiles, words, e):
             nc.sync.dma_start(out=tiles[e].bitcast(I32), in_=words.rearrange("e s p n -> (e s) p n")[e].bitcast(I32))
 
-        def load_scales(tile, scales):
+        def load_scales(tile, scales, lo, hi):
             rows = scales.rearrange("e s (q r) n -> r q (e s) n", r=SCALE_ROWS)
             for r in range(SCALE_ROWS):
-                nc.sync.dma_start(out=tile[r:P:QUADRANT, :, :].bitcast(I32), in_=rows[r].bitcast(I32))
+                nc.sync.dma_start(out=tile[r:P:QUADRANT, :, :].bitcast(I32), in_=rows[r][:, lo:hi, :].bitcast(I32))
 
         def load_gate(columns, lo, hi):
             nc.sync.dma_start(out=columns, in_=gate[0:P, lo:hi])
 
-        for tile in (s1_sb, s3_sb, s2_sb):
+        for tile in (s1_halves[0], s3_all, s1_halves[1], s2_sb):
             nc.vector.memset(tile[:].rearrange("p a n -> p (a n)").bitcast(I32), 0)
         nc.gpsimd.memset(warm[:, 0:1], 0.0)
         nc.scalar.activation(out=warm[:, 1:2], in_=warm[:, 0:1], func=SILU)
@@ -97,17 +98,19 @@ def tile_moe_pre_glu_silu_kernel(
             nc.sync.dma_start(out=x_rows[d][:], in_=x_by_d[d])
         load_first_words(w1_sb, w1_words, 0)
         nc.sync.dma_start(pos1_sb[:], pos1)
-        load_scales(s1_sb, w1_scales)
+        load_scales(s1_halves[0], w1_scales, 0, 2)
         load_gate(gate_of[1], C, 2 * C)
         load_first_words(w3_sb, w3_words, 0)
-        load_scales(s3_sb, w3_scales)
+        load_scales(s3_all, w3_scales, 0, E)
         load_first_words(w1_sb, w1_words, 1)
         load_gate(gate_late[:], 2 * C, SLOTS)
         load_first_words(w3_sb, w3_words, 1)
         load_words(w1_late[:], w1_words, 2, E)
-        load_words(w3_late[:], w3_words, 2, E)
+        load_scales(s1_halves[1], w1_scales, 2, E)
+        for e in range(2, E):
+            load_first_words(w3_sb, w3_words, e)
         load_words(w2_sb[:], w2_words, 0, E * H_PASSES)
-        load_scales(s2_sb, w2_scales)
+        load_scales(s2_sb, w2_scales, 0, E * H_PASSES)
         nc.sync.dma_start(pos2_sb[:], pos2)
         make_identity(nc, identity[:])
 
@@ -162,11 +165,11 @@ def tile_moe_pre_glu_silu_kernel(
         def finish_on_vector(e, x_bf16, end):
             for lo in range(0, end, P):
                 gather_weighted(e, PACK - 1, lo, lo + P)
-            if end < C:
-                weigh_share(x_bf16)
             for lo in range(0, end, P):
                 round_x(x_bf16, lo, lo + P)
-            for c in (range(TILES_PER_EXPERT) if end == C else reversed(range(TILES_PER_EXPERT))):
+            if end < C:
+                weigh_share(x_bf16)
+            for c in range(TILES_PER_EXPERT):
                 quantise_x(x_bf16[:, c * PASS:(c + 1) * PASS], TILES_PER_EXPERT * e + c, 1)
 
         def first_product(unit, words, scales, bank):
@@ -176,7 +179,7 @@ def tile_moe_pre_glu_silu_kernel(
             nc.tensor.matmul_mx(
                 out=sums[:], lhsT=x_mx[j][0], lhsT_scale=x_mx[j][1],
                 rhs=words[e][:, 2 * PASS * s:2 * PASS * (s + 1)].bitcast(FP4X4),
-                rhs_scale=scales[:, e, PASS * s:PASS * (s + 1)], start=True, stop=True,
+                rhs_scale=scales[e][:, PASS * s:PASS * (s + 1)], start=True, stop=True,
             )
             return sums[:].rearrange("j (p u v) -> j u p v", u=2, v=2)
 
@@ -192,7 +195,7 @@ def tile_moe_pre_glu_silu_kernel(
 
         def multiply(unit, behind=None):
             if behind is None:
-                h = work.tile([P, PASS], BF16, name="h", tag="h%d" % unit)
+                h = work.tile([P, PASS], BF16, name="h", tag="h%d" % unit, align_bytes=256)
             else:
                 h = chain.tile([P, PASS], BF16, name="h%d" % unit, align_bytes=256, offset=behind * STEP)
             nc.vector.tensor_tensor(h[:].rearrange("j (u p v) -> j u p v", u=2, v=2), act_of[unit], b_of[unit], MULT)
@@ -212,7 +215,7 @@ def tile_moe_pre_glu_silu_kernel(
 
         def turn_expert(e, first_bank):
             words = open_turned("turned%d" % e, H_PASSES, C)
-            banks = (first_bank, bank_of[UNITS_PER_EXPERT * e + 3])
+            banks = (first_bank, bank_of[(3, 8, 11)[e]])
             for c in range(TILES_PER_EXPERT):
                 first = UNITS_PER_EXPERT * e + H_PASSES * c
                 turn([first, first + 1], banks[c], words[:, :, c * P:(c + 1) * P, :])
@@ -276,19 +279,19 @@ def tile_moe_pre_glu_silu_kernel(
         activate(11, "a0")
         linear(11, bank_of[3])
         multiply(7)
-        turn_expert(1, "a1")
         multiply(8)
+        turn_expert(1, "a1")
         multiply(9)
-        quantise_x(x_bf16[:], 6, 2, "act8")
+        quantise_x(x_bf16[:], 6, 2, "act9")
         activate(12, "a2")
-        linear(12, bank_of[8])
+        linear(12, bank_of[7])
         multiply(10)
         activate(13, "a0")
         linear(13, bank_of[9])
         activate(14, "a1")
         linear(14, bank_of[10])
         activate(15, "a2")
-        linear(15, bank_of[7])
+        linear(15, bank_of[8])
         multiply(11, behind=3)
         h0_codes = chain.tile([P, H_PASSES * C], U32, name="h0_codes", align_bytes=256, offset=E * STEP)
         turn_expert(2, "a0")

@@ -213,9 +213,8 @@ def tile_moe_pre_glu_silu_kernel(
             turned_of[name] = tile
             return tile[:].bitcast(F32).rearrange("p (s c u) -> p s c u", s=passes, u=2)
 
-        def turn_expert(e, first_bank):
+        def turn_expert(e, banks):
             words = open_turned("turned%d" % e, H_PASSES, C)
-            banks = (first_bank, bank_of[(3, 8, 11)[e]])
             for c in range(TILES_PER_EXPERT):
                 first = UNITS_PER_EXPERT * e + H_PASSES * c
                 turn([first, first + 1], banks[c], words[:, :, c * P:(c + 1) * P, :])
@@ -264,7 +263,7 @@ def tile_moe_pre_glu_silu_kernel(
         linear(6, "b3")
         linear(7, bank_of[2])
         multiply(3)
-        turn_expert(0, "a2")
+        turn_expert(0, ("a2", bank_of[3]))
         multiply(4)
         quantise_x(x_bf16[:], 4, 2, "act3")
         x_bf16 = weigh_and_round(3)
@@ -279,22 +278,22 @@ def tile_moe_pre_glu_silu_kernel(
         activate(11, "a0")
         linear(11, bank_of[3])
         multiply(7)
+        turn_expert(1, ("a1", "a2"))
         multiply(8)
-        turn_expert(1, "a1")
         multiply(9)
-        quantise_x(x_bf16[:], 6, 2, "act9")
-        activate(12, "a2")
-        linear(12, bank_of[7])
+        quantise_x(x_bf16[:], 6, 2, "act8")
+        activate(12, bank_of[7])
+        linear(12, bank_of[8])
         multiply(10)
         activate(13, "a0")
         linear(13, bank_of[9])
         activate(14, "a1")
         linear(14, bank_of[10])
-        activate(15, "a2")
-        linear(15, bank_of[8])
+        activate(15, bank_of[7])
+        linear(15, "a2")
         multiply(11, behind=3)
         h0_codes = chain.tile([P, H_PASSES * C], U32, name="h0_codes", align_bytes=256, offset=E * STEP)
-        turn_expert(2, "a0")
+        turn_expert(2, ("a0", bank_of[11]))
         h0 = quantise_h("turned0", H_PASSES, C, codes=h0_codes)
         h1 = quantise_h("turned1", H_PASSES, C, tag="act11")
         multiply(12)
@@ -314,7 +313,7 @@ def tile_moe_pre_glu_silu_kernel(
         second_product(y_mid[:, C:C + P], 3, quantise_h("turned6", H_PASSES, P))
         nc.scalar.copy(out=y_sb[:, 2 * C:3 * C + P], in_=y_mid[:])
         h7 = quantise_h("turned14", 1, P) + quantise_h("turned15", 1, P)
-        y_last = psum.tile([P, P], F32, name="y_last", tag="a2")
+        y_last = psum.tile([P, P], F32, name="y_last", tag=bank_of[7])
         second_product(y_last[:], 3, h7)
         nc.vector.tensor_copy(out=y_sb[:, 3 * C + P:SLOTS], in_=y_last[:])
 

@@ -59,12 +59,14 @@ def tile_moe_pre_glu_silu_kernel(
         gate_of = [plain_last[:, 1, :], keep.tile([P, C], F32, name="gate1")[:]] + [gate_late[:, c * C:(c + 1) * C] for c in range(2)]
         w1_late = keep.tile([P, 2, 2 * H], U8, name="w1_late", align_bytes=256)
         w1_sb = [keep.tile([P, 2 * H], U8, name="w1_sb%d" % e, align_bytes=256)[:] for e in range(2)] + [w1_late[:, e, :] for e in range(2)]
-        w3_sb = [keep.tile([P, 2 * H], U8, name="w3_sb%d" % e, align_bytes=256)[:] for e in range(E)]
+        w3_sb = [keep.tile([P, 2 * H], U8, name="w3_sb%d" % e, align_bytes=256)[:] for e in range(2)]
         w2_sb = keep.tile([P, E * H_PASSES, 2 * N], U8, name="w2_sb", align_bytes=256)
         s1_halves = [keep.tile([P, E // 2, H], U8, name="s1_half%d" % c, align_bytes=256) for c in range(2)]
         s1_sb = [s1_halves[e // 2][:, e % 2, :] for e in range(E)]
-        s3_all = keep.tile([P, E, H], U8, name="s3_all", align_bytes=256)
-        s3_sb = [s3_all[:, e, :] for e in range(E)]
+        s3_halves = [keep.tile([P, E // 2, H], U8, name="s3_half%d" % c, align_bytes=256) for c in range(2)]
+        s3_sb = [s3_halves[e // 2][:, e % 2, :] for e in range(E)]
+        w3_late = keep.tile([P, 2, 2 * H], U8, name="w3_late", align_bytes=256)
+        w3_sb.extend(w3_late[:, e, :] for e in range(2))
         s2_sb = keep.tile([P, E * H_PASSES, N], U8, name="s2_sb", align_bytes=256)
         identity = keep.tile([P, P], F32, name="identity", align_bytes=256)
         y_sb = keep.tile([P, SLOTS], F32, name="y_sb")
@@ -77,15 +79,15 @@ def tile_moe_pre_glu_silu_kernel(
         def load_first_words(tiles, words, e):
             nc.sync.dma_start(out=tiles[e].bitcast(I32), in_=words.rearrange("e s p n -> (e s) p n")[e].bitcast(I32))
 
-        def load_scales(tile, scales, lo, hi):
+        def load_scales(tile, scales, lo, hi, which=range(SCALE_ROWS)):
             rows = scales.rearrange("e s (q r) n -> r q (e s) n", r=SCALE_ROWS)
-            for r in range(SCALE_ROWS):
+            for r in which:
                 nc.sync.dma_start(out=tile[r:P:QUADRANT, :, :].bitcast(I32), in_=rows[r][:, lo:hi, :].bitcast(I32))
 
         def load_gate(columns, lo, hi):
             nc.sync.dma_start(out=columns, in_=gate[0:P, lo:hi])
 
-        for tile in (s1_halves[0], s3_all, s1_halves[1], s2_sb):
+        for tile in (s1_halves[0], s3_halves[0], s1_halves[1], s3_halves[1], s2_sb):
             nc.vector.memset(tile[:].rearrange("p a n -> p (a n)").bitcast(I32), 0)
         nc.gpsimd.memset(warm[:, 0:1], 0.0)
         nc.scalar.activation(out=warm[:, 1:2], in_=warm[:, 0:1], func=SILU)
@@ -101,14 +103,15 @@ def tile_moe_pre_glu_silu_kernel(
         load_scales(s1_halves[0], w1_scales, 0, 2)
         load_gate(gate_of[1], C, 2 * C)
         load_first_words(w3_sb, w3_words, 0)
-        load_scales(s3_all, w3_scales, 0, E)
+        load_scales(s3_halves[0], w3_scales, 0, 2)
         load_first_words(w1_sb, w1_words, 1)
         load_gate(gate_late[:], 2 * C, SLOTS)
         load_first_words(w3_sb, w3_words, 1)
         load_words(w1_late[:], w1_words, 2, E)
-        load_scales(s1_halves[1], w1_scales, 2, E)
-        for e in range(2, E):
-            load_first_words(w3_sb, w3_words, e)
+        load_words(w3_late[:], w3_words, 2, E)
+        for r in range(SCALE_ROWS):
+            load_scales(s1_halves[1], w1_scales, 2, E, [r])
+            load_scales(s3_halves[1], w3_scales, 2, E, [r])
         load_words(w2_sb[:], w2_words, 0, E * H_PASSES)
         load_scales(s2_sb, w2_scales, 0, E * H_PASSES)
         nc.sync.dma_start(pos2_sb[:], pos2)

@@ -45,6 +45,7 @@ def tile_moe_pre_glu_silu_kernel(
         keep = ctx.enter_context(tc.tile_pool(name="keep", bufs=1))
         work = ctx.enter_context(tc.tile_pool(name="work", bufs=1))
         chain = ctx.enter_context(tc.tile_pool(name="chain", bufs=1))
+        late = ctx.enter_context(tc.tile_pool(name="late", bufs=1))
         psum = ctx.enter_context(tc.psum_pool(name="psum", bufs=1))
 
         offs_sb = keep.tile([P, SLOTS // PER_COLUMN], U16, name="offs_sb")
@@ -69,7 +70,6 @@ def tile_moe_pre_glu_silu_kernel(
         w3_sb.extend(w3_late[:, e, :] for e in range(2))
         s2_sb = keep.tile([P, E * H_PASSES, N], U8, name="s2_sb", align_bytes=256)
         identity = keep.tile([P, P], F32, name="identity", align_bytes=256)
-        y_sb = keep.tile([P, SLOTS], F32, name="y_sb")
         warm = keep.tile([P, 2], F32, name="warm")
 
         def load_words(tile, words, lo, hi):
@@ -211,8 +211,11 @@ def tile_moe_pre_glu_silu_kernel(
                     nc.tensor.transpose(bank[:, s, u, :], h_of[unit][:, u * P:(u + 1) * P], identity[:])
             nc.scalar.copy(out=target, in_=bank[:].rearrange("p s u c -> p s c u"))
 
-        def open_turned(name, passes, slots):
-            tile = work.tile([P, passes * slots * PACK], BF16, name=name, align_bytes=256)
+        def open_turned(name, passes, slots, under_y=False):
+            if under_y:
+                tile = late.tile([P, passes * slots * PACK], BF16, name=name, align_bytes=256, offset=0)
+            else:
+                tile = work.tile([P, passes * slots * PACK], BF16, name=name, align_bytes=256)
             turned_of[name] = tile
             return tile[:].bitcast(F32).rearrange("p (s c u) -> p s c u", s=passes, u=2)
 
@@ -306,18 +309,21 @@ def tile_moe_pre_glu_silu_kernel(
         multiply(13)
         turn([12, 13], bank_of[13], open_turned("turned6", H_PASSES, P))
         multiply(14)
-        nc.scalar.copy(out=y_sb[:, 0:2 * C], in_=y_first[:])
-        turn([14], bank_of[14], open_turned("turned14", 1, P))
+        turn([14], bank_of[14], open_turned("turned14", 1, P, under_y=True))
         multiply(15)
         turn([15], bank_of[15], open_turned("turned15", 1, P))
         h2 = quantise_h("turned2", H_PASSES, C, tag="act14")
-        y_mid = psum.tile([P, C + P], F32, name="y_mid", tag="a0")
-        second_product(y_mid[:, 0:C], 2, h2)
-        second_product(y_mid[:, C:C + P], 3, quantise_h("turned6", H_PASSES, P))
-        nc.scalar.copy(out=y_sb[:, 2 * C:3 * C + P], in_=y_mid[:])
+        y_mid = psum.tile([P, C], F32, name="y_mid", tag="a0")
+        second_product(y_mid[:], 2, h2)
+        y_six = psum.tile([P, P], F32, name="y_six", tag=bank_of[12])
+        second_product(y_six[:], 3, quantise_h("turned6", H_PASSES, P))
         h7 = quantise_h("turned14", 1, P) + quantise_h("turned15", 1, P)
         y_last = psum.tile([P, P], F32, name="y_last", tag=bank_of[7])
         second_product(y_last[:], 3, h7)
+        y_sb = late.tile([P, SLOTS], F32, name="y_sb", align_bytes=256, offset=0)
+        nc.scalar.copy(out=y_sb[:, 0:2 * C], in_=y_first[:])
+        nc.vector.tensor_copy(out=y_sb[:, 2 * C:3 * C], in_=y_mid[:])
+        nc.scalar.copy(out=y_sb[:, 3 * C:3 * C + P], in_=y_six[:])
         nc.vector.tensor_copy(out=y_sb[:, 3 * C + P:SLOTS], in_=y_last[:])
 
         cuts = (0, 160, 352, T)

@@ -18,6 +18,10 @@ QUADRANT = 32
 SCALE_ROWS = 4
 
 SHARE = 128
+PLAIN = SHARE + 2 * C
+WINDOW = PLAIN + 32
+TILE_ORDER = (0, 1, 3, 2, 4, 5, 6, 7)
+FILL = 192
 STEP = 2 * PASS
 
 FLOPS = 2 * SLOTS * (2 * K * H + H * N)
@@ -51,13 +55,12 @@ def tile_moe_pre_glu_silu_kernel(
         offs_sb = keep.tile([P, SLOTS // PER_COLUMN], U16, name="offs_sb")
         pos1_sb = keep.tile([P, T // PER_COLUMN], U16, name="pos1_sb")
         pos2_sb = keep.tile([P, T // PER_COLUMN], U16, name="pos2_sb")
-        x_rows = [keep.tile([P, T], F32, name="x_rows%d" % d) for d in range(PACK)]
+        x_rows = [keep.tile([P, WINDOW], F32, name="x_rows%d" % d) for d in range(PACK)]
         weighted = keep.tile([P, PACK, C], F32, name="weighted")
-        plain_first = keep.tile([P, PACK, SHARE + C], F32, name="plain_first")
-        plain_last = keep.tile([P, PACK, C], F32, name="plain_last")
-        staged = {2: plain_first[:, :, SHARE:], 3: plain_last[:]}
+        plain = keep.tile([P, PACK, PLAIN + C - FILL], F32, name="plain")
+        staged = {e: plain[:, :, SHARE + (e - 2) * C:SHARE + (e - 1) * C] for e in (2, 3)}
         gate_late = keep.tile([P, 2 * C], F32, name="gate_late")
-        gate_of = [plain_last[:, 1, :], keep.tile([P, C], F32, name="gate1")[:]] + [gate_late[:, c * C:(c + 1) * C] for c in range(2)]
+        gate_of = [plain[:, 1, PLAIN - FILL:PLAIN - FILL + C], keep.tile([P, C], F32, name="gate1")[:]] + [gate_late[:, c * C:(c + 1) * C] for c in range(2)]
         w1_late = keep.tile([P, 2, 2 * H], U8, name="w1_late", align_bytes=256)
         w1_sb = [keep.tile([P, 2 * H], U8, name="w1_sb%d" % e, align_bytes=256)[:] for e in range(2)] + [w1_late[:, e, :] for e in range(2)]
         w3_sb = [keep.tile([P, 2 * H], U8, name="w3_sb%d" % e, align_bytes=256)[:] for e in range(2)]
@@ -87,17 +90,19 @@ def tile_moe_pre_glu_silu_kernel(
         def load_gate(columns, lo, hi):
             nc.sync.dma_start(out=columns, in_=gate[0:P, lo:hi])
 
+        for d in range(PACK):
+            nc.gpsimd.memset(x_rows[d][:, T:], 0.0)
         for tile in (s1_halves[0], s3_halves[0], s1_halves[1], s3_halves[1], s2_sb):
             nc.vector.memset(tile[:].rearrange("p a n -> p (a n)").bitcast(I32), 0)
         nc.gpsimd.memset(warm[:, 0:1], 0.0)
         nc.scalar.activation(out=warm[:, 1:2], in_=warm[:, 0:1], func=SILU)
 
         x_by_d = xT.rearrange("(p d) t -> d p t", d=PACK)
-        nc.sync.dma_start(out=x_rows[0][:], in_=x_by_d[0])
+        nc.sync.dma_start(out=x_rows[0][:, :T], in_=x_by_d[0])
         nc.sync.dma_start(offs_sb[:], offs)
         load_gate(gate_of[0], 0, C)
         for d in range(1, PACK):
-            nc.sync.dma_start(out=x_rows[d][:], in_=x_by_d[d])
+            nc.sync.dma_start(out=x_rows[d][:, :T], in_=x_by_d[d])
         load_first_words(w1_sb, w1_words, 0)
         nc.sync.dma_start(pos1_sb[:], pos1)
         load_scales(s1_halves[0], w1_scales, 0, 2)
@@ -132,8 +137,8 @@ def tile_moe_pre_glu_silu_kernel(
         def gather_weighted(e, d, lo, hi):
             nc.vector.tensor_tensor(weighted[:, d, lo:hi], tokens(d, e * C + lo, e * C + hi), gate_of[e][:, lo:hi], MULT)
 
-        def gather_scalar(rows, d, lo, hi):
-            nc.scalar.activation(rows[:, d, :], tokens(d, lo, hi), COPY)
+        def gather_scalar(d, count):
+            nc.scalar.activation(plain[:, d, :count], tokens(d, SLOTS - PLAIN, SLOTS - PLAIN + count), COPY)
 
         def open_x(e):
             return chain.tile([P, C * PACK], BF16, name="x_bf16_%d" % e, align_bytes=256, offset=e * STEP)
@@ -161,26 +166,27 @@ def tile_moe_pre_glu_silu_kernel(
             weights = gate_of[1][:, C - SHARE:].rearrange("p (c two) -> p c two", two=2).unsqueeze(2)
             nc.vector.tensor_tensor(
                 x_bf16[:, (C - SHARE) * PACK:].rearrange("p (c two d) -> p c d two", two=2, d=PACK),
-                plain_first[:, :, :SHARE].rearrange("p d (c two) -> p c d two", two=2),
+                plain[:, :, :SHARE].rearrange("p d (c two) -> p c d two", two=2),
                 weights.to_broadcast([P, SHARE // 2, PACK, 2]), MULT,
             )
 
         def finish_on_vector(e, x_bf16, end):
             for lo in range(0, end, P):
                 gather_weighted(e, PACK - 1, lo, lo + P)
-            for lo in range(0, end, P):
-                round_x(x_bf16, lo, lo + P)
             if end < C:
                 weigh_share(x_bf16)
-            for c in range(TILES_PER_EXPERT):
-                quantise_x(x_bf16[:, c * PASS:(c + 1) * PASS], TILES_PER_EXPERT * e + c, 1)
+            for lo in range(0, end, P):
+                round_x(x_bf16, lo, lo + P)
+            for j in TILE_ORDER[TILES_PER_EXPERT * e:TILES_PER_EXPERT * (e + 1)]:
+                c = j % TILES_PER_EXPERT
+                quantise_x(x_bf16[:, c * PASS:(c + 1) * PASS], j, 1)
 
         def first_product(unit, words, scales, bank):
             j, s = divmod(unit, H_PASSES)
             e = j // TILES_PER_EXPERT
             sums = psum.tile([P, PASS], F32, name="sums", tag=bank)
             nc.tensor.matmul_mx(
-                out=sums[:], lhsT=x_mx[j][0], lhsT_scale=x_mx[j][1],
+                out=sums[:], lhsT=x_mx[TILE_ORDER[j]][0], lhsT_scale=x_mx[TILE_ORDER[j]][1],
                 rhs=words[e][:, 2 * PASS * s:2 * PASS * (s + 1)].bitcast(FP4X4),
                 rhs_scale=scales[e][:, PASS * s:PASS * (s + 1)], start=True, stop=True,
             )
@@ -223,7 +229,8 @@ def tile_moe_pre_glu_silu_kernel(
             words = open_turned("turned%d" % e, H_PASSES, C)
             for c in range(TILES_PER_EXPERT):
                 first = UNITS_PER_EXPERT * e + H_PASSES * c
-                turn([first, first + 1], banks[c], words[:, :, c * P:(c + 1) * P, :])
+                place = TILE_ORDER[TILES_PER_EXPERT * e + c] % TILES_PER_EXPERT
+                turn([first, first + 1], banks[c], words[:, :, place * P:(place + 1) * P, :])
 
         def quantise_h(name, passes, slots, tag=None, codes=None):
             codes, scales = quantise(turned_of[name][:], passes * slots, "h" + name, tag, codes)
@@ -237,16 +244,13 @@ def tile_moe_pre_glu_silu_kernel(
                 )
 
         for d in range(PACK):
-            gather_scalar(plain_first, d, 2 * C - SHARE, 3 * C)
-        nc.vector.tensor_copy(plain_last[:, 0, 0:P], tokens(0, 3 * C, 3 * C + P))
-        nc.scalar.activation(plain_last[:, 0, P:C], tokens(0, 3 * C + P, SLOTS), COPY)
-        for d in range(2, PACK):
-            gather_scalar(plain_last, d, 3 * C, SLOTS)
+            gather_scalar(d, PLAIN - (P, FILL, 0, 0)[d])
+        nc.vector.tensor_copy(plain[:, 0, PLAIN - P:PLAIN], tokens(0, SLOTS - P, SLOTS))
         for d in range(PACK - 1):
             gather_weighted(0, d, 0, C)
         x_bf16 = open_x(0)
         finish_on_vector(0, x_bf16, C)
-        nc.vector.tensor_copy(plain_last[:, 1, :], tokens(1, 3 * C, SLOTS))
+        nc.vector.tensor_copy(plain[:, 1, PLAIN - FILL:PLAIN], tokens(1, SLOTS - FILL, SLOTS))
         for d in range(PACK - 1):
             gather_weighted(1, d, 0, C - SHARE)
         finish_on_vector(1, open_x(1), C - SHARE)

@@ -59,8 +59,8 @@ def tile_moe_pre_glu_silu_kernel(
         weighted = keep.tile([P, PACK, C], F32, name="weighted")
         plain = keep.tile([P, PACK, PLAIN + C - FILL], F32, name="plain")
         staged = {e: plain[:, :, SHARE + (e - 2) * C:SHARE + (e - 1) * C] for e in (2, 3)}
-        gate_late = keep.tile([P, 2 * C], F32, name="gate_late")
-        gate_of = [plain[:, 1, PLAIN - FILL:PLAIN - FILL + C], keep.tile([P, C], F32, name="gate1")[:]] + [gate_late[:, c * C:(c + 1) * C] for c in range(2)]
+        gate_mid = keep.tile([P, 2 * C], F32, name="gate_mid")
+        gate_of = [plain[:, 1, PLAIN - FILL:PLAIN - FILL + C], gate_mid[:, :C], gate_mid[:, C:], keep.tile([P, C], F32, name="gate3")[:]]
         w1_late = keep.tile([P, 2, 2 * H], U8, name="w1_late", align_bytes=256)
         w1_sb = [keep.tile([P, 2 * H], U8, name="w1_sb%d" % e, align_bytes=256)[:] for e in range(2)] + [w1_late[:, e, :] for e in range(2)]
         w3_sb = [keep.tile([P, 2 * H], U8, name="w3_sb%d" % e, align_bytes=256)[:] for e in range(2)]
@@ -106,14 +106,14 @@ def tile_moe_pre_glu_silu_kernel(
         load_first_words(w1_sb, w1_words, 0)
         nc.sync.dma_start(pos1_sb[:], pos1)
         load_scales(s1_halves[0], w1_scales, 0, 2)
-        load_gate(gate_of[1], C, 2 * C)
+        load_gate(gate_mid[:], C, 3 * C)
         load_first_words(w3_sb, w3_words, 0)
         load_scales(s3_halves[0], w3_scales, 0, 2)
         load_first_words(w1_sb, w1_words, 1)
-        load_gate(gate_late[:], 2 * C, SLOTS)
         load_first_words(w3_sb, w3_words, 1)
         load_words(w1_late[:], w1_words, 2, E)
         load_words(w3_late[:], w3_words, 2, E)
+        load_gate(gate_of[3], 3 * C, SLOTS)
         for r in range(SCALE_ROWS):
             load_scales(s1_halves[1], w1_scales, 2, E, [r])
             load_scales(s3_halves[1], w3_scales, 2, E, [r])

from contextlib import ExitStack

import concourse.mybir as mybir
from concourse.masks import make_identity

K, T, E, C, H, N = 512, 512, 4, 256, 1024, 128
SLOTS = E * C
P = 128
PACK = 4
PASS = P * PACK
H_PASSES = H // PASS
TILES_PER_EXPERT = C // P
UNITS_PER_EXPERT = TILES_PER_EXPERT * H_PASSES
TILES = SLOTS // P
UNITS = TILES * H_PASSES
PER_COLUMN = 16
QUADRANT = 32
SCALE_ROWS = 4

SHARE = 128
PLAIN = SHARE + 2 * C
WINDOW = PLAIN + 32
TILE_ORDER = (0, 1, 3, 2, 4, 5, 6, 7)
FILL = 192
STEP = 2 * PASS

FLOPS = 2 * SLOTS * (2 * K * H + H * N)
BYTES = 4 * K * T + 4 * P * SLOTS + E * (2 * K * H + H * N) * 17 // 32 + 2 * P * (SLOTS + 2 * T) // PER_COLUMN + 4 * N * T

F32 = mybir.dt.float32
BF16 = mybir.dt.bfloat16
I32 = mybir.dt.int32
U32 = mybir.dt.uint32
U16 = mybir.dt.uint16
U8 = mybir.dt.uint8
FP8X4 = mybir.dt.float8_e4m3fn_x4
FP4X4 = mybir.dt.float4_e2m1fn_x4
MULT = mybir.AluOpType.mult
ADD = mybir.AluOpType.add
SILU = mybir.ActivationFunctionType.Silu
COPY = mybir.ActivationFunctionType.Copy


def tile_moe_pre_glu_silu_kernel(
    tc, xT, w1_words, w1_scales, w3_words, w3_scales, w2_words, w2_scales, gate, offs, pos1, pos2, out
):
    nc = tc.nc
    with ExitStack() as ctx:
        keep = ctx.enter_context(tc.tile_pool(name="keep", bufs=1))
        work = ctx.enter_context(tc.tile_pool(name="work", bufs=1))
        chain = ctx.enter_context(tc.tile_pool(name="chain", bufs=1))
        late = ctx.enter_context(tc.tile_pool(name="late", bufs=1))
        psum = ctx.enter_context(tc.psum_pool(name="psum", bufs=1))

        offs_sb = keep.tile([P, SLOTS // PER_COLUMN], U16, name="offs_sb")
        pos1_sb = keep.tile([P, T // PER_COLUMN], U16, name="pos1_sb")
        pos2_sb = keep.tile([P, T // PER_COLUMN], U16, name="pos2_sb")
        x_rows = [keep.tile([P, WINDOW], F32, name="x_rows%d" % d) for d in range(PACK)]
        weighted = keep.tile([P, PACK, C], F32, name="weighted")
        plain = keep.tile([P, PACK, PLAIN + C - FILL], F32, name="plain")
        staged = {e: plain[:, :, SHARE + (e - 2) * C:SHARE + (e - 1) * C] for e in (2, 3)}
        gate_mid = keep.tile([P, 2 * C], F32, name="gate_mid")
        gate_of = [plain[:, 1, PLAIN - FILL:PLAIN - FILL + C], gate_mid[:, :C], gate_mid[:, C:], keep.tile([P, C], F32, name="gate3")[:]]
        w1_late = keep.tile([P, 2, 2 * H], U8, name="w1_late", align_bytes=256)
        w1_sb = [keep.tile([P, 2 * H], U8, name="w1_sb%d" % e, align_bytes=256)[:] for e in range(2)] + [w1_late[:, e, :] for e in range(2)]
        w3_sb = [keep.tile([P, 2 * H], U8, name="w3_sb%d" % e, align_bytes=256)[:] for e in range(2)]
        w2_sb = keep.tile([P, E * H_PASSES, 2 * N], U8, name="w2_sb", align_bytes=256)
        s1_halves = [keep.tile([P, E // 2, H], U8, name="s1_half%d" % c, align_bytes=256) for c in range(2)]
        s1_sb = [s1_halves[e // 2][:, e % 2, :] for e in range(E)]
        s3_halves = [keep.tile([P, E // 2, H], U8, name="s3_half%d" % c, align_bytes=256) for c in range(2)]
        s3_sb = [s3_halves[e // 2][:, e % 2, :] for e in range(E)]
        w3_late = keep.tile([P, 2, 2 * H], U8, name="w3_late", align_bytes=256)
        w3_sb.extend(w3_late[:, e, :] for e in range(2))
        s2_sb = keep.tile([P, E * H_PASSES, N], U8, name="s2_sb", align_bytes=256)
        identity = keep.tile([P, P], F32, name="identity", align_bytes=256)
        warm = keep.tile([P, 2], F32, name="warm")

        def load_words(tile, words, lo, hi):
            by_pass = words.rearrange("e s p n -> p (e s) n")
            nc.sync.dma_start(out=tile.bitcast(I32), in_=by_pass[:, lo:hi, :].bitcast(I32))

        def load_first_words(tiles, words, e):
            nc.sync.dma_start(out=tiles[e].bitcast(I32), in_=words.rearrange("e s p n -> (e s) p n")[e].bitcast(I32))

        def load_scales(tile, scales, lo, hi, which=range(SCALE_ROWS)):
            rows = scales.rearrange("e s (q r) n -> r q (e s) n", r=SCALE_ROWS)
            for r in which:
                nc.sync.dma_start(out=tile[r:P:QUADRANT, :, :].bitcast(I32), in_=rows[r][:, lo:hi, :].bitcast(I32))

        def load_gate(columns, lo, hi):
            nc.sync.dma_start(out=columns, in_=gate[0:P, lo:hi])

        for d in range(PACK):
            nc.gpsimd.memset(x_rows[d][:, T:], 0.0)
        for tile in (s1_halves[0], s3_halves[0], s1_halves[1], s3_halves[1], s2_sb):
            nc.vector.memset(tile[:].rearrange("p a n -> p (a n)").bitcast(I32), 0)
        nc.gpsimd.memset(warm[:, 0:1], 0.0)
        nc.scalar.activation(out=warm[:, 1:2], in_=warm[:, 0:1], func=SILU)

        x_by_d = xT.rearrange("(p d) t -> d p t", d=PACK)
        nc.sync.dma_start(out=x_rows[0][:, :T], in_=x_by_d[0])
        nc.sync.dma_start(offs_sb[:], offs)
        load_gate(gate_of[0], 0, C)
        for d in range(1, PACK):
            nc.sync.dma_start(out=x_rows[d][:, :T], in_=x_by_d[d])
        load_first_words(w1_sb, w1_words, 0)
        nc.sync.dma_start(pos1_sb[:], pos1)
        load_scales(s1_halves[0], w1_scales, 0, 2)
        load_gate(gate_mid[:], C, 3 * C)
        load_first_words(w3_sb, w3_words, 0)
        load_scales(s3_halves[0], w3_scales, 0, 2)
        load_first_words(w1_sb, w1_words, 1)
        load_first_words(w3_sb, w3_words, 1)
        load_words(w1_late[:], w1_words, 2, E)
        load_words(w3_late[:], w3_words, 2, E)
        load_gate(gate_of[3], 3 * C, SLOTS)
        for r in range(SCALE_ROWS):
            load_scales(s1_halves[1], w1_scales, 2, E, [r])
            load_scales(s3_halves[1], w3_scales, 2, E, [r])
        load_words(w2_sb[:], w2_words, 0, E * H_PASSES)
        load_scales(s2_sb, w2_scales, 0, E * H_PASSES)
        nc.sync.dma_start(pos2_sb[:], pos2)
        make_identity(nc, identity[:])

        x_mx, act_of, b_of, h_of, turned_of, h_mx, bank_of = {}, {}, {}, {}, {}, {}, {}

        def quantise(values, width, name, tag=None, codes=None):
            if codes is None:
                codes = work.tile([P, width], U32, name=name + "_codes", tag=tag or name + "_codes", align_bytes=256)
            scales = work.tile([P, width], U8, name=name + "_scales", align_bytes=256)
            nc.vector.quantize_mx(out=codes[:].bitcast(FP8X4), scales=scales[:], in_=values)
            return codes, scales

        def tokens(d, lo, hi):
            return x_rows[d][:].indirect(offs_sb[:, lo // PER_COLUMN:hi // PER_COLUMN])

        def gather_weighted(e, d, lo, hi):
            nc.vector.tensor_tensor(weighted[:, d, lo:hi], tokens(d, e * C + lo, e * C + hi), gate_of[e][:, lo:hi], MULT)

        def gather_scalar(d, count):
            nc.scalar.activation(plain[:, d, :count], tokens(d, SLOTS - PLAIN, SLOTS - PLAIN + count), COPY)

        def open_x(e):
            return chain.tile([P, C * PACK], BF16, name="x_bf16_%d" % e, align_bytes=256, offset=e * STEP)

        def round_x(x_bf16, lo, hi):
            nc.vector.tensor_copy(
                out=x_bf16[:, lo * PACK:hi * PACK].rearrange("p (c two d) -> p c d two", two=2, d=PACK),
                in_=weighted[:, :, lo:hi].rearrange("p d (c two) -> p c d two", two=2),
            )

        def weigh_and_round(e):
            x_bf16 = open_x(e)
            nc.gpsimd.tensor_tensor(
                x_bf16[:].rearrange("p (c d) -> p c d", d=PACK), staged[e].rearrange("p d c -> p c d"),
                gate_of[e].unsqueeze(2).to_broadcast([P, C, PACK]), MULT,
            )
            return x_bf16

        def quantise_x(values, first, count, tag=None):
            codes, scales = quantise(values, count * P, "x%d" % first, tag)
            for c in range(count):
                x_mx[first + c] = (codes[:, c * P:(c + 1) * P].bitcast(FP8X4), scales[:, c * P:(c + 1) * P])

        def weigh_share(x_bf16):
            weights = gate_of[1][:, C - SHARE:].rearrange("p (c two) -> p c two", two=2).unsqueeze(2)
            nc.vector.tensor_tensor(
                x_bf16[:, (C - SHARE) * PACK:].rearrange("p (c two d) -> p c d two", two=2, d=PACK),
                plain[:, :, :SHARE].rearrange("p d (c two) -> p c d two", two=2),
                weights.to_broadcast([P, SHARE // 2, PACK, 2]), MULT,
            )

        def finish_on_vector(e, x_bf16, end):
            for lo in range(0, end, P):
                gather_weighted(e, PACK - 1, lo, lo + P)
            if end < C:
                weigh_share(x_bf16)
            for lo in range(0, end, P):
                round_x(x_bf16, lo, lo + P)
            for j in TILE_ORDER[TILES_PER_EXPERT * e:TILES_PER_EXPERT * (e + 1)]:
                c = j % TILES_PER_EXPERT
                quantise_x(x_bf16[:, c * PASS:(c + 1) * PASS], j, 1)

        def first_product(unit, words, scales, bank):
            j, s = divmod(unit, H_PASSES)
            e = j // TILES_PER_EXPERT
            sums = psum.tile([P, PASS], F32, name="sums", tag=bank)
            nc.tensor.matmul_mx(
                out=sums[:], lhsT=x_mx[TILE_ORDER[j]][0], lhsT_scale=x_mx[TILE_ORDER[j]][1],
                rhs=words[e][:, 2 * PASS * s:2 * PASS * (s + 1)].bitcast(FP4X4),
                rhs_scale=scales[e][:, PASS * s:PASS * (s + 1)], start=True, stop=True,
            )
            return sums[:].rearrange("j (p u v) -> j u p v", u=2, v=2)

        def activate(unit, bank=None):
            sums = first_product(unit, w1_sb, s1_sb, bank or "a%d" % (unit % 3))
            act = work.tile([P, PASS], F32, name="act", tag="act%d" % unit, align_bytes=256)
            act_of[unit] = act[:].rearrange("j (u p v) -> j u p v", u=2, v=2)
            nc.scalar.activation(out=act_of[unit], in_=sums, func=SILU)

        def linear(unit, bank):
            bank_of[unit] = bank
            b_of[unit] = first_product(unit, w3_sb, s3_sb, bank)

        def multiply(unit, behind=None):
            if behind is None:
                h = work.tile([P, PASS], BF16, name="h", tag="h%d" % unit, align_bytes=256)
            else:
                h = chain.tile([P, PASS], BF16, name="h%d" % unit, align_bytes=256, offset=behind * STEP)
            nc.vector.tensor_tensor(h[:].rearrange("j (u p v) -> j u p v", u=2, v=2), act_of[unit], b_of[unit], MULT)
            h_of[unit] = h[:].bitcast(F32)

        def turn(units, bank_tag, target):
            bank = psum.tile([P, len(units), 2, P], F32, name="turn_bank", tag=bank_tag)
            for s, unit in enumerate(units):
                for u in range(2):
                    nc.tensor.transpose(bank[:, s, u, :], h_of[unit][:, u * P:(u + 1) * P], identity[:])
            nc.scalar.copy(out=target, in_=bank[:].rearrange("p s u c -> p s c u"))

        def open_turned(name, passes, slots, under_y=False):
            if under_y:
                tile = late.tile([P, passes * slots * PACK], BF16, name=name, align_bytes=256, offset=0)
            else:
                tile = work.tile([P, passes * slots * PACK], BF16, name=name, align_bytes=256)
            turned_of[name] = tile
            return tile[:].bitcast(F32).rearrange("p (s c u) -> p s c u", s=passes, u=2)

        def turn_expert(e, banks):
            words = open_turned("turned%d" % e, H_PASSES, C)
            for c in range(TILES_PER_EXPERT):
                first = UNITS_PER_EXPERT * e + H_PASSES * c
                place = TILE_ORDER[TILES_PER_EXPERT * e + c] % TILES_PER_EXPERT
                turn([first, first + 1], banks[c], words[:, :, place * P:(place + 1) * P, :])

        def quantise_h(name, passes, slots, tag=None, codes=None):
            codes, scales = quantise(turned_of[name][:], passes * slots, "h" + name, tag, codes)
            return [(codes[:, s * slots:(s + 1) * slots].bitcast(FP8X4), scales[:, s * slots:(s + 1) * slots]) for s in range(passes)]

        def second_product(columns, e, operands):
            for s, (codes, scales) in enumerate(operands):
                nc.tensor.matmul_mx(
                    out=columns, lhsT=w2_sb[:, e * H_PASSES + s, :].bitcast(FP4X4), lhsT_scale=s2_sb[:, e * H_PASSES + s, :],
                    rhs=codes, rhs_scale=scales, start=(s == 0), stop=(s == H_PASSES - 1),
                )

        for d in range(PACK):
            gather_scalar(d, PLAIN - (P, FILL, 0, 0)[d])
        nc.vector.tensor_copy(plain[:, 0, PLAIN - P:PLAIN], tokens(0, SLOTS - P, SLOTS))
        for d in range(PACK - 1):
            gather_weighted(0, d, 0, C)
        x_bf16 = open_x(0)
        finish_on_vector(0, x_bf16, C)
        nc.vector.tensor_copy(plain[:, 1, PLAIN - FILL:PLAIN], tokens(1, SLOTS - FILL, SLOTS))
        for d in range(PACK - 1):
            gather_weighted(1, d, 0, C - SHARE)
        finish_on_vector(1, open_x(1), C - SHARE)
        x_bf16 = weigh_and_round(2)
        for unit in range(3):
            activate(unit)
        activate(3, "b4")
        for unit in range(3):
            linear(unit, "b%d" % unit)
        activate(4, "b3")
        multiply(0)
        linear(3, bank_of[0])
        activate(5)
        multiply(1)
        activate(6)
        linear(4, "b4")
        multiply(2)
        activate(7)
        linear(5, bank_of[1])
        linear(6, "b3")
        linear(7, bank_of[2])
        multiply(3)
        turn_expert(0, ("a2", bank_of[3]))
        multiply(4)
        quantise_x(x_bf16[:], 4, 2, "act3")
        x_bf16 = weigh_and_round(3)
        activate(8, "a0")
        linear(8, bank_of[4])
        multiply(5)
        activate(9, "a1")
        linear(9, bank_of[5])
        multiply(6, behind=2)
        activate(10, "a2")
        linear(10, bank_of[6])
        activate(11, "a0")
        linear(11, bank_of[3])
        multiply(7)
        turn_expert(1, ("a1", "a2"))
        multiply(8)
        multiply(9)
        quantise_x(x_bf16[:], 6, 2, "act8")
        activate(12, bank_of[7])
        linear(12, bank_of[8])
        multiply(10)
        activate(13, "a0")
        linear(13, bank_of[9])
        activate(14, "a1")
        linear(14, bank_of[10])
        activate(15, bank_of[7])
        linear(15, "a2")
        multiply(11, behind=3)
        h0_codes = chain.tile([P, H_PASSES * C], U32, name="h0_codes", align_bytes=256, offset=E * STEP)
        turn_expert(2, ("a0", bank_of[11]))
        h0 = quantise_h("turned0", H_PASSES, C, codes=h0_codes)
        h1 = quantise_h("turned1", H_PASSES, C, tag="act11")
        multiply(12)
        y_first = psum.tile([P, 2 * C], F32, name="y_first", tag="a1")
        second_product(y_first[:, 0:C], 0, h0)
        second_product(y_first[:, C:2 * C], 1, h1)
        multiply(13)
        turn([12, 13], bank_of[13], open_turned("turned6", H_PASSES, P))
        multiply(14)
        turn([14], bank_of[14], open_turned("turned14", 1, P, under_y=True))
        multiply(15)
        turn([15], bank_of[15], open_turned("turned15", 1, P))
        h2 = quantise_h("turned2", H_PASSES, C, tag="act14")
        y_mid = psum.tile([P, C], F32, name="y_mid", tag="a0")
        second_product(y_mid[:], 2, h2)
        y_six = psum.tile([P, P], F32, name="y_six", tag=bank_of[12])
        second_product(y_six[:], 3, quantise_h("turned6", H_PASSES, P))
        h7 = quantise_h("turned14", 1, P) + quantise_h("turned15", 1, P)
        y_last = psum.tile([P, P], F32, name="y_last", tag=bank_of[7])
        second_product(y_last[:], 3, h7)
        y_sb = late.tile([P, SLOTS], F32, name="y_sb", align_bytes=256, offset=0)
        nc.scalar.copy(out=y_sb[:, 0:2 * C], in_=y_first[:])
        nc.vector.tensor_copy(out=y_sb[:, 2 * C:3 * C], in_=y_mid[:])
        nc.scalar.copy(out=y_sb[:, 3 * C:3 * C + P], in_=y_six[:])
        nc.vector.tensor_copy(out=y_sb[:, 3 * C + P:SLOTS], in_=y_last[:])

        cuts = (0, 160, 352, T)
        pieces = [slice(cuts[c], cuts[c + 1]) for c in range(3)]
        columns = [slice(s.start // PER_COLUMN, s.stop // PER_COLUMN) for s in pieces]
        y1 = [work.tile([P, s.stop - s.start], F32, name="y1_%d" % s.start) for s in pieces]
        total = [work.tile([P, s.stop - s.start], F32, name="total%d" % s.start) for s in pieces]
        y2 = work.tile([P, T - cuts[2]], F32, name="y2")
        for c in range(3):
            nc.scalar.activation(y1[c][:], y_sb[:].indirect(pos1_sb[:, columns[c]]), COPY)
        nc.vector.tensor_copy(y2[:], y_sb[:].indirect(pos2_sb[:, columns[2]]))
        for c in range(2):
            nc.vector.tensor_tensor(total[c][:], y_sb[:].indirect(pos2_sb[:, columns[c]]), y1[c][:], ADD)
        nc.vector.tensor_tensor(total[2][:], y2[:], y1[2][:], ADD)
        for c in range(3):
            nc.sync.dma_start(out=out[:, pieces[c]], in_=total[c][:])
